import numpy as np, ml_dtypes
CORES = [5,29,101,125,133,157,229,253]
N = 8
BF = ml_dtypes.bfloat16
M, S, B, L, CAP, MISS, FILL, LN = 768, 3072, 2048, 4, 128, 384, 2304, 3
def split(s):
    t = (13 * s) >> 2
    return t & (N - 1), (t >> LN) & (B - 1)
def first(c):
    k = np.ascontiguousarray(c, np.uint8).view(np.uint64); o = np.lexsort((k[:, 1], k[:, 0])); same = np.all(k[o[1:]] == k[o[:-1]], axis=1)
    m = np.ones(len(k), bool); m[o[1:][same]] = False; return m
def weights(rng, kind):
    w = 2 * rng.integers(0, 128, (8, 16)) + 1; w[:, :4] = 2 * rng.integers(64, 128, (8, 4)) + 1
    if kind == "near": return np.tile(np.repeat(np.array([109, 185]), 8), (8, 1))
    if kind == "spread": w[:, 4:] = rng.choice(np.array([1, 3, 255]), (8, 12))
    return rng.permuted(w, axis=1)
def pool(rng, n, kind):
    if kind == "spread": c = (1 + np.floor(255 * rng.random((n, 16)) ** 6)).astype(np.uint8)
    else: c = rng.integers(2, 255, (n, 16), dtype=np.uint8) if kind == "near" else rng.integers(1, 256, (n, 16), dtype=np.uint8)
    if kind != "near": c[0] = 1; c[1] = 255
    return c[first(c)]
def counts(rng, kind, top):
    cnt = np.zeros((N, N), np.int64)
    for r in range(N):
        if kind == "full":
            q = rng.permutation(N); left = M
            for e in [top] + [int(x) for x in q if x != top]:
                cnt[r, e] = min(CAP, left); left -= min(CAP, left)
        else:
            v = rng.multinomial(M, np.full(N, 2.0 ** -LN))
            while np.max(v) > CAP:
                i = np.argmax(v); e = v[i] - CAP; v[i] = CAP; v[np.argmin(v)] += e
            cnt[r] = v
    return cnt
def alter(rng, ch, wg, m):
    lift = (294 - wg).astype(np.uint8); can = ch <= 255 - lift
    u = np.flatnonzero((((13 * (ch.astype(np.int64) @ wg)) & 3) != 3) & np.any(can, axis=1))[:m // 2]
    one = ch[u]; i = np.argmax(np.where(can[u], rng.random((len(u), 16)), -1.0), axis=1); one[np.arange(len(u)), i] += lift[i]
    two = ch[:m - len(u)].copy(); a = np.arange(len(two))
    i = rng.permuted(np.tile(np.arange(8), (len(two), 1)), axis=1)[:, :2] + 8 * rng.integers(0, 2, (len(two), 1)); two[a, i[:, 0]] += 1; two[a, i[:, 1]] -= 1
    return np.concatenate([two, one])
def make(rng, kind):
    w = weights(rng, kind); chunks = np.zeros((N, 8, 16, M), np.uint8); store = np.zeros((N, 8, 16, S), np.uint8)
    head = np.zeros((N, 8, B), np.int32); follow = np.zeros((N, 8, S), np.int32); vac = np.zeros((N, 8, MISS), np.int32)
    for g in range(8):
        c = pool(rng, N * (3 * FILL // 2 + 2 * MISS), kind); own, buc = split(c.astype(np.int64) @ w[g])
        key = own * B + buc; o = np.argsort(key, kind="stable"); ks = key[o]; rk = np.zeros(len(c), np.int64); rk[o] = np.arange(len(c)) - np.searchsorted(ks, ks)
        top = int(rng.integers(0, N)); cnt = counts(rng, kind, top); parts = [[] for r in range(N)]; stored = np.zeros(len(c), bool)
        for q in range(N):
            mine = np.flatnonzero(own == q); st = mine[rk[mine] < L][:FILL]; stored[st] = True; rest = rng.permutation(mine[~stored[mine]])
            pl = rng.permutation(S - 1) + 1; at = pl[:FILL]; vac[q, g] = pl[FILL:FILL + MISS]; store[q, g][:, at] = c[st].T
            tab = np.zeros((B, L + 1), np.int64); tab[buc[st], rk[st]] = at; head[q, g] = tab[:, 0]; follow[q, g][at] = tab[buc[st], rk[st] + 1]
            n = int(np.sum(cnt[:, q])); h = rng.permutation(FILL)
            if kind == "full": m = MISS if q == top else int(rng.integers(0, MISS + 1))
            elif kind == "deep": m = 0 if (q + g) % 2 else int(rng.integers(1, MISS + 1))
            else: m = int(rng.integers(MISS // 4, MISS + 1))
            m = min(m, n)
            if kind == "deep":
                h = h[np.argsort(-rk[st[h]], kind="stable")]; rest = rest[np.argsort(-np.count_nonzero(tab, axis=1)[buc[rest]], kind="stable")]
            if kind == "near": new = alter(rng, c[st[h]], w[g], m)
            else: new = c[rest[:m]]
            both = np.concatenate([new, c[st[h[:n - m]]]]); e = np.add.accumulate(cnt[:, q])
            if kind == "full" and q == top: both = np.roll(both, CAP * int(rng.integers(0, N)), axis=0)
            else: both = rng.permutation(both)
            for r in range(N): parts[r].append(both[e[r] - cnt[r, q]:e[r]])
        for r in range(N): chunks[r, g] = rng.permutation(np.concatenate(parts[r])).T
    return {"chunks": chunks.reshape(N, 128, M).astype(np.float32).astype(BF), "store": store.reshape(N, 128, S).astype(np.float32).astype(BF), "head": head, "follow": follow, "vac": vac,
            "wt": np.broadcast_to(w.reshape(128, 1), (N, 128, 1)).astype(np.float32)}
def setup_inputs(rng):
    return make(rng, "plain")
def setup_inputs_full(rng):
    return make(rng, "full")
def setup_inputs_near(rng):
    return make(rng, "near")
def setup_inputs_deep(rng):
    return make(rng, "deep")
def setup_inputs_spread(rng):
    return make(rng, "spread")
def whole(v, lo, hi):
    return bool(np.all((v >= lo) & (v <= hi) & (v == np.floor(v))))
def check_inputs(d):
    c, s, w = [np.asarray(d[k]).astype(np.float32) for k in ("chunks", "store", "wt")]; head, follow, vac = [np.asarray(d[k]).astype(np.int64) for k in ("head", "follow", "vac")]; bad = []
    if not whole(w, 1, 255) or not np.all(2 * np.floor(w * 0.5) != w) or not np.all(w == w[:1]): bad.append("weights")
    if not whole(c, 1, 255): bad.append("symbols")
    if not whole(s, 0, 255): bad.append("store")
    for k, v in (("head", head), ("follow", follow), ("vac", vac)):
        if not whole(v, 0, S - 1): bad.append(k)
    if bad: return bad
    c = c.astype(np.int64).reshape(N, 8, 16, M); s = s.astype(np.int64).reshape(N, 8, 16, S); w = w[0].astype(np.int64).reshape(8, 16)
    full = np.all(s > 0, axis=2); empty = np.all(s == 0, axis=2)
    if not np.all(full | empty) or np.any(full[:, :, 0]): bad.append("store")
    if np.any(follow[empty] != 0): bad.append("follow of an empty place")
    for g in range(8):
        for q in range(N):
            so, sb = split(w[g] @ s[q, g]); p = head[q, g]; seen = np.zeros(S, np.int64); ok = True
            for step in range(L):
                b = np.flatnonzero(p > 0); e = p[b]; ok = ok and bool(np.all(full[q, g][e] & (so[e] == q) & (sb[e] == b)))
                seen += np.bincount(e, minlength=S); p = follow[q, g][p]
            if not ok or np.any(p != 0) or not np.array_equal(seen, full[q, g].astype(np.int64)): bad.append("chains")
            v = vac[q, g]
            if len(np.unique(v)) != MISS or np.any(v == 0) or not np.all(empty[q, g][v]): bad.append("vacant places")
        nc = c[:, g].transpose(0, 2, 1).reshape(-1, 16); sc = s[:, g].transpose(0, 2, 1).reshape(-1, 16)[full[:, g].reshape(-1)]
        own = split(nc @ w[g])[0]; m = first(np.concatenate([sc, nc])); miss = m[len(sc):]
        if not np.all(m[:len(sc)]): bad.append("stored chunks differ")
        if not np.all(first(nc)): bad.append("new chunks differ")
        for q in range(N):
            if np.max(np.count_nonzero(own.reshape(N, M) == q, axis=1)) > CAP: bad.append("chunks of a pair")
            if np.count_nonzero(miss & (own == q)) > MISS: bad.append("misses")
    return sorted(set(bad))
def reference(chunks, store, head, follow, vac, wt):
    y = np.zeros((N, 8, M), np.float32); z = np.array(store)
    for g in range(8):
        raw = np.ascontiguousarray(chunks[:, 16 * g:16 * g + 16].transpose(1, 0, 2)).reshape(16, N * M)
        c = raw.astype(np.float32).astype(np.int64); own, buc = split(wt[0, 16 * g:16 * g + 16, 0].astype(np.int64) @ c); res = np.zeros(N * M, np.int64)
        for q in range(N):
            st = store[q, 16 * g:16 * g + 16].astype(np.float32).astype(np.int64); j = np.flatnonzero(own == q); v = c[:, j]
            p = head[q, g][buc[j]].astype(np.int64); ans = np.zeros(len(j), np.int64)
            for step in range(L):
                ans = np.where((p > 0) & np.all(st[:, p] == v, axis=0), p, ans); p = follow[q, g][p].astype(np.int64)
            miss = np.flatnonzero(ans == 0); new = vac[q, g][:len(miss)].astype(np.int64)
            ans[miss] = new; z[q, 16 * g:16 * g + 16][:, new] = raw[:, j[miss]]
            res[j] = q * S + ans
        y[:, g] = res.reshape(N, M)
    return {"y": y, "z": z}

@@ -1,0 +1,389 @@
+from concourse.bass import DstId, RemoteDMATransfer
+from concourse.mybir import AluOpType as A, ActivationFunctionType as F
+
+N, M, S, B, CAP, MISS = 8, 768, 3072, 2048, 128, 384
+W = N * CAP
+VB = S + W
+NCS, NDS = 60, 24
+
+SCRATCH = {
+    "ch": ("sbuf", [128, M], "bfloat16"), "wc": ("sbuf", [128, 1], "float32"),
+    "st": ("sbuf", [128, VB + N * MISS], "bfloat16"),
+    "hd": ("sbuf", [128, 128], "int32"), "fo": ("sbuf", [128, 192], "int32"), "va": ("sbuf", [128, 24], "int32"),
+    "ones": ("sbuf", [128, 256], "bfloat16"), "mones": ("sbuf", [128, 128], "bfloat16"),
+    "xs": ("sbuf", [128, W], "bfloat16"), "fw": ("sbuf", [128, S], "bfloat16"), "rm": ("sbuf", [128, 384], "bfloat16"),
+    "d1": ("sbuf", [128, 144], "bfloat16"), "dd": ("sbuf", [128, 144], "bfloat16"), "zw": ("sbuf", [128, 144], "bfloat16"),
+    "zf": ("sbuf", [128, 144], "bfloat16"), "zi": ("sbuf", [128, 144], "bfloat16"), "zo": ("sbuf", [128, 144], "bfloat16"),
+    "z1": ("sbuf", [128, 144], "bfloat16"), "z1f": ("sbuf", [128, 144], "float32"),
+    "nb": ("sbuf", [128, 128], "bfloat16"), "nt": ("sbuf", [128, 128], "bfloat16"), "ntt": ("sbuf", [128, 128], "bfloat16"),
+    "nw": ("sbuf", [128, 128], "bfloat16"),
+    "ident": ("sbuf", [128, 128], "bfloat16"), "identf": ("sbuf", [128, 128], "float32"),
+    "kq": ("sbuf", [128, 384], "bfloat16"), "pcol": ("sbuf", [128, 1], "float32"),
+    "idhi": ("sbuf", [128, 256], "bfloat16"), "idlo": ("sbuf", [128, 256], "bfloat16"),
+    "fhb": ("sbuf", [128, 192], "bfloat16"), "flb": ("sbuf", [128, 192], "bfloat16"),
+    "l0": ("sbuf", [128, 128], "uint16"), "l1": ("sbuf", [128, 128], "uint16"),
+    "vf": ("sbuf", [128, 24 * N], "float32"), "vl": ("sbuf", [128, 24 * N], "int32"),
+    "x1": ("sbuf", [128, 48], "int32"), "own": ("sbuf", [128, 48], "int32"),
+    "mk": ("sbuf", [128, 384], "bfloat16"), "sm": ("sbuf", [128, 384], "bfloat16"), "dm": ("sbuf", [128, 384], "float16"),
+    "ld": ("sbuf", [128, 48], "uint16"),
+    "cc": ("sbuf", [128, W], "bfloat16"),
+    "taba": ("sbuf", [128, B], "bfloat16"), "tabb": ("sbuf", [128, B], "bfloat16"),
+    "g0": ("sbuf", [128, B], "bfloat16"), "g1": ("sbuf", [128, B], "bfloat16"),
+    "jr": ("sbuf", [128, 64], "int32"), "ja": ("sbuf", [128, 64], "int32"), "ji": ("sbuf", [128, 64], "float32"),
+    "x2": ("sbuf", [128, 64], "int32"), "ba": ("sbuf", [128, 64], "int32"), "bb": ("sbuf", [128, 64], "int32"),
+    "bc": ("sbuf", [128, 64], "int32"), "lb": ("sbuf", [128, 64], "uint16"),
+    "l2": ("sbuf", [128, 64], "uint16"), "l3": ("sbuf", [128, 64], "uint16"),
+    "tag": ("sbuf", [128, W], "bfloat16"), "tbg": ("sbuf", [128, W], "bfloat16"), "t3g": ("sbuf", [128, W], "bfloat16"),
+    "ne0": ("sbuf", [128, W], "bfloat16"), "ne1": ("sbuf", [128, W], "bfloat16"),
+    "ne2": ("sbuf", [128, W], "bfloat16"), "ne3": ("sbuf", [128, W], "bfloat16"),
+    "t2s": ("sbuf", [128, 64], "float32"), "t3s": ("sbuf", [128, 64], "float32"),
+    "mm": ("sbuf", [128, 64], "float32"), "rr": ("sbuf", [128, 64], "float32"), "m0": ("sbuf", [128, 64], "float32"),
+    "mo": ("sbuf", [128, 64], "float32"), "uu": ("sbuf", [128, 64], "float32"),
+    "ms": ("sbuf", [128, 64], "bfloat16"), "s2": ("sbuf", [128, 64], "bfloat16"),
+    "ix": ("sbuf", [128, 64], "uint16"), "lv": ("sbuf", [128, 24], "uint16"), "an": ("sbuf", [128, 64], "uint16"),
+    "yw": ("sbuf", [128, VB + N * MISS], "float32"),
+    "ay": ("sbuf", [128, W], "float32"), "yb": ("sbuf", [128, M], "float32"),
+    "h1": ("sbuf", [128, 2 * CAP], "bfloat16"), "h2": ("sbuf", [128, 64], "uint16"),
+    "p0": ("psum", [128, 512], "float32"), "p1": ("psum", [128, 512], "float32"),
+    "p2": ("psum", [128, 512], "float32"), "p3": ("psum", [128, 512], "float32"),
+    "p4": ("psum", [128, 512], "float32"), "p5": ("psum", [128, 512], "float32"),
+    "p6": ("psum", [128, 512], "float32"), "p7": ("psum", [128, 512], "float32"),
+}
+SEMAPHORES = (["ls", "rv", "rc", "rn", "rf", "qv", "qc", "qa"]
+              + ["c%d" % i for i in range(NCS)] + ["d%d" % i for i in range(NDS)])
+
+
+def bits(engines):
+    m = 0
+    for e in engines:
+        m |= 1 << e
+    return m
+
+
+def share(engines, n):
+    k = 1
+    while 2 * k * n <= len(engines):
+        k *= 2
+    out = [engines[i * k:(i + 1) * k] for i in range(n)]
+    if len(engines) - n * k >= k:
+        out[-1] = out[-1] + engines[n * k:(n + 1) * k]
+    return out
+
+
+def layout(cores, r, topo):
+    c = cores[r]
+    near = [q for q in range(N) if q != r and topo.may_write(c, cores[q])]
+    far = [q for q in range(N) if q != r and q not in near]
+    cand = sorted([h for h in topo.cores_of(c) if h not in cores], key=lambda h: (topo.die(h) != topo.die(c), h))
+    helpers = [h for h in cand if all(topo.may_write(h, cores[q]) for q in far)][:2]
+    helpers.append([h for h in cand if h not in helpers and all(topo.may_write(h, cores[q]) for q in near)][0])
+    on = topo.engines(c, helpers[0])
+    half = len(far) // 2
+    jobs = [far[:half], far[half:], near]
+    return {"near": near, "far": far, "helpers": helpers, "jobs": jobs, "order": far + near + [r],
+            "e_near": share(topo.engines(c, cores[near[0]]), len(near)), "e_on": share(on, 2), "e_vac": share(on, 3),
+            "e_help": [share(topo.engines(helpers[k], cores[jobs[k][0]]), len(jobs[k])) for k in range(3)]}
+
+
+def xfer(topo, src_core, dst_core, engines, sem, src, dst):
+    rid, pid = topo.addr(dst_core, src_core)
+    return RemoteDMATransfer(dst_ids=[DstId(rid=rid, pnc=pid)], dma_engine_mask=bits(engines), remote_sem=sem, src=src, dst=dst)
+
+
+def helper_program(g, core, T, topo, lay, r, k):
+    cores, me = T.cores, lay[r]
+    job, eng = me["jobs"][k], me["e_help"][k]
+    g.wait_ge(T.sem.qv, len(me["e_vac"][k]))
+    g.remote_dma_fused([xfer(topo, core, cores[q], eng[j], T.sem.rv, T.va[:, :], T.vl[:, 24 * r:24 * r + 24])
+                        for j, q in enumerate(job)], local_sem=T.sem.ls)
+    if k == 2:
+        g.wait_ge(T.sem.ls, sum(len(e) for e in eng))
+        return
+    got = len(me["e_on"][k])
+    g.wait_ge(T.sem.qc, got)
+    g.remote_dma_fused([xfer(topo, core, cores[q], eng[j], T.sem.rc, T.h1[:, CAP * j:CAP * j + CAP], T.cc[:, CAP * r:CAP * r + CAP])
+                        for j, q in enumerate(job)], local_sem=T.sem.ls)
+    g.wait_ge(T.sem.qa, got)
+    tr = []
+    for j, q in enumerate(job):
+        a, b = 8 * (q - job[0]), 8 * lay[q]["order"].index(r)
+        tr.append(xfer(topo, core, cores[q], eng[j], T.sem.rf, T.h2[:, a:a + 8], T.an[:, b:b + 8]))
+    g.remote_dma_fused(tr, local_sem=T.sem.ls)
+    g.wait_ge(T.sem.ls, 3 * sum(len(e) for e in eng))
+
+
+def emit(ops, queues, T):
+    known = {q: set() for q in queues}
+    snap, waits, needed = [], [], set()
+    for i, o in enumerate(ops):
+        kn, w = known[o["q"]], []
+        for d in sorted(set(o["deps"]), reverse=True):
+            if d not in kn:
+                w.append(d)
+                kn.add(d)
+                kn |= snap[d]
+        needed.update(w)
+        waits.append(w)
+        snap.append(set(kn) if o["q"] else set())
+    pools = {True: [], False: []}
+    sig = {}
+    for i, o in enumerate(ops):
+        if o["q"] is None:
+            sig[i] = o["ext"]
+            continue
+        q = queues[o["q"]]
+        for d in waits[i]:
+            q.wait_ge(T.sem[sig[d][0]], sig[d][1])
+        slot = None
+        if i in needed:
+            pool = pools[o["dma"]]
+            for s in pool:
+                if s[1] in snap[i]:
+                    slot = s
+                    break
+            if slot is None:
+                slot = [("d%d" if o["dma"] else "c%d") % len(pool), i, 0]
+                pool.append(slot)
+            slot[1] = i
+        for n, fn in enumerate(o["fns"]):
+            ins = fn()
+            if slot is not None and (not o["acc"] or n == len(o["fns"]) - 1):
+                inc = 16 if o["dma"] else 1
+                ins.then_inc(T.sem[slot[0]], inc)
+                slot[2] += inc
+        if slot is not None:
+            sig[i] = (slot[0], slot[2])
+
+
+def rank_program(g, core, T, topo):
+    cores = T.cores
+    lay = [layout(cores, r, topo) for r in range(N)]
+    r = T.rank_of(core)
+    if r is None:
+        for q in range(N):
+            if core in lay[q]["helpers"]:
+                helper_program(g, core, T, topo, lay, q, lay[q]["helpers"].index(core))
+        return
+    me = lay[r]
+    order, near, far = me["order"], me["near"], me["far"]
+    V, Sc, PE, Sy = g.vector, g.scalar, g.tensor, g.sync
+    queues = {"g": g, "v": V, "s": Sc, "p": PE, "y": Sy, None: None}
+    ops = []
+
+    def op(q, fns, deps=(), dma=False, acc=False):
+        ops.append({"q": q, "fns": fns if isinstance(fns, list) else [fns], "deps": list(deps), "dma": dma, "acc": acc})
+        return len(ops) - 1
+
+    def ext(name, val):
+        ops.append({"q": None, "fns": [], "deps": [], "ext": (name, val)})
+        return len(ops) - 1
+
+    def dma(q, out, in_, deps=()):
+        return op(q, lambda: queues[q].dma_start(out, in_), deps, dma=True)
+
+    def ts(out, in0, s1, op0, deps, s2=None, op1=None):
+        if op1 is None:
+            return op("v", lambda: V.tensor_scalar(out, in0, s1, None, op0), deps)
+        return op("v", lambda: V.tensor_scalar(out, in0, s1, s2, op0, op1), deps)
+
+    def tt(out, in0, in1, o, deps):
+        return op("v", lambda: V.tensor_tensor(out, in0, in1, o), deps)
+
+    def cp(out, in_, deps):
+        return op("v", lambda: V.tensor_copy(out, in_), deps)
+
+    def scan(out, d0, d1, init, o1, deps):
+        return op("v", lambda: V.tensor_tensor_scan(out, d0, d1, init, A.mult, o1), deps)
+
+    def fill(ap, val, deps=()):
+        return op("v", lambda: V.memset(ap, val), deps)
+
+    def act(out, in_, deps, func=F.Copy, **kw):
+        return op("s", lambda: Sc.activation(out, in_, func, **kw), deps)
+
+    def sel(out, in_, pattern, cmp, fillv, base, cm, deps):
+        return op("g", lambda: g.affine_select(out, in_, pattern, cmp, fillv, base, cm), deps)
+
+    def iota(out, pattern, base, cm, deps=(), flt=True):
+        if flt:
+            return op("g", lambda: g.iota(out, pattern, base, cm, allow_small_or_imprecise_dtypes=True), deps)
+        return op("g", lambda: g.iota(out, pattern, base, cm), deps)
+
+    def mm(out, lhsT, rhs, start, stop):
+        return lambda: PE.matmul(out, lhsT, rhs, start, stop)
+
+    def wrap(out, z, src, n, deps, start=True, stop=True, before=(), a0=0):
+        fns = list(before) + [mm(out, z[:, 15 - i:143 - i], src[:, a0 + i:a0 + n:16], start and i == 0, stop and i == 15) for i in range(16)]
+        return op("p", fns, deps, acc=True)
+
+    def remote(transfers, deps):
+        return op("g", lambda: g.remote_dma_fused(transfers, local_sem=T.sem.ls), deps)
+
+    def landing(key, k, senders):
+        return sum(len(lay[q][key][k][lay[q]["jobs"][k].index(r)]) for q in senders if r in lay[q]["jobs"][k])
+
+    n_near = sum(len(lay[q]["e_near"][lay[q]["near"].index(r)]) for q in near)
+    n_far = landing("e_help", 0, far) + landing("e_help", 1, far)
+    x_v = ext("rv", n_far + landing("e_help", 2, near))
+    x_c, x_n, x_f = ext("rc", n_near + n_far), ext("rn", n_near), ext("rf", n_far)
+    x_l = ext("ls", sum(len(e) for e in me["e_vac"]) + 2 * (sum(len(e) for e in me["e_near"]) + sum(len(e) for e in me["e_on"])))
+
+    l_va = dma("y", T.vl[:, 24 * r:24 * r + 24], T.vac[:, :])
+    l_wt = dma("s", T.wc[:, :], T.wt[:, :])
+    l_ch = dma("y", T.ch[:, :], T.chunks[:, :])
+    l_fo = dma("s", T.fo[:, :], T.follow[:, :])
+    l_hd = dma("s", T.hd[:, :], T.head[:, :])
+
+    k_one = fill(T.ones[:, :], 1.0)
+    k_mon = fill(T.mones[:, :], -1.0)
+    k_idlo = scan(T.idlo[:, :], T.ones[:, :], T.ones[:, :], -1.0, A.add, [k_one])
+    k_rm0 = fill(T.rm[:, :], 1.0)
+    k_fw = fill(T.fw[:, :], 1.0)
+    k_rm = fill(T.rm[:, 0:384:48], 0.0, [k_rm0])
+    last = [[-16, 9], [256, 16]]
+    upto = [[16, 9], [0, 16]]
+    k_pc = iota(T.pcol[:, :], [[0, 1]], 0, 256)
+    k_d1 = sel(T.d1[:, :], T.ones[:, 0:144], last, A.is_ge, 0.0, -3840, 1, [k_one])
+    k_nt0 = sel(T.nt[:, :], T.mones[:, :], [[-1, 128]], A.is_ge, 0.0, 0, 1, [k_mon])
+    k_dd = sel(T.dd[:, :], T.d1[:, :], upto, A.is_ge, 0.0, 15, -1, [k_d1])
+    k_nt = sel(T.nt[:, :], T.nt[:, :], [[16, 8], [0, 16]], A.is_ge, 0.0, 15, -1, [k_nt0])
+    k_idhi = act(T.idhi[:, :], T.ones[:, :], [k_one, k_pc], F.Identity, bias=T.pcol[:, :], scale=0.0)
+    k_xs = op("s", [(lambda a=a: Sc.activation(T.xs[:, a:a + 256], T.ones[:, :], F.Copy, scale=-1.0)) for a in range(0, W, 256)], [k_one])
+    k_kq = op("s", [(lambda b=b: Sc.activation(T.kq[:, 48 * b:48 * b + 48], T.ones[:, 0:48], F.Copy, scale=-8.0 * b)) for b in range(N)], [k_one])
+    k_yv = op("s", [(lambda a=a: Sc.activation(T.yw[:, VB + a:VB + a + W], T.xs[:, :], F.Copy)) for a in range(0, N * MISS, W)], [k_xs])
+    k_ntt = op("v", lambda: V.transpose(T.ntt[:, :], T.nt[:, :]), [k_nt])
+    k_zw = ts(T.zw[:, :], T.dd[:, :], T.wc[:, :], A.mult, [k_dd, l_wt])
+    k_nb = tt(T.nb[:, :], T.nt[:, :], T.ntt[:, :], A.min, [k_ntt])
+    k_id = tt(T.ident[:, :], T.nt[:, :], T.ntt[:, :], A.mult, [k_ntt])
+
+    remote([xfer(topo, core, me["helpers"][k], me["e_vac"][k], T.sem.qv, T.vl[:, 24 * r:24 * r + 24], T.va[:, :]) for k in range(3)], [l_va])
+    k_zf = sel(T.zf[:, :], T.d1[:, :], upto, A.is_ge, 0.0, 1, -1, [k_d1])
+
+    a1 = cp(T.fhb[:, :], T.fo[:, :], [l_fo])
+    w_id = op("y", [lambda: Sy.dma_start(T.fw[3:128:16, :], T.idlo[0:96, :]), lambda: Sy.dma_start(T.fw[2:128:16, :], T.idhi[0:96, :])],
+              [k_fw, k_idlo, k_idhi], dma=True)
+    m_s1 = wrap(T.p0[:, 0:48], T.zw, T.ch, M, [k_zw, l_ch])
+    a2 = tt(T.flb[:, :], T.fo[:, :], T.fhb[:, :], A.subtract, [a1])
+    w_fo = op("y", [lambda: Sy.dma_start(T.fw[0:128:16, :], T.fhb[:, :]), lambda: Sy.dma_start(T.fw[1:128:16, :], T.flb[:, :])],
+              [k_fw, a1, a2], dma=True)
+    l_st = dma("y", T.st[:, 0:S], T.store[:, :])
+    b1 = ts(T.x1[:, :], T.p0[:, 0:48], 13.0, A.mult, [m_s1])
+    b2 = ts(T.own[:, :], T.x1[:, :], 2, A.arith_shift_right, [b1], 7, A.bitwise_and)
+    b3 = op("v", [(lambda b=b: V.tensor_scalar(T.mk[:, 48 * b:48 * b + 48], T.own[:, :], float(order[b]), None, A.is_equal)) for b in range(N)], [b2])
+    b4 = scan(T.sm[:, :], T.rm[:, :], T.mk[:, :], 0.0, A.subtract, [b3, k_rm])
+    c_l0 = cp(T.l0[:, :], T.hd[:, :], [l_hd])
+    op("p", mm(T.p1[:, 0:384], T.nb[:, :], T.kq[:, :], True, False), [k_nb, k_kq])
+    op("p", mm(T.p1[:, 0:384], T.nt[:, :], T.mk[:, :], False, False), [k_nt, b3])
+    m_pos = op("p", mm(T.p1[:, 0:384], T.nb[:, :], T.sm[:, :], False, True), [b4])
+    b5 = tt(T.dm[:, :], T.p1[:, 0:384], T.mk[:, :], A.mult, [m_pos])
+    m_de = op("p", [mm(T.p2[:, 0:48], T.ident[:, :], T.dm[:, 48 * b:48 * b + 48], b == 0, b == N - 1) for b in range(N)], [b5, k_id], acc=True)
+    b6 = cp(T.ld[:, :], T.p2[:, 0:48], [m_de])
+    b7 = cp(T.xs[:, :].indirect(T.ld[:, :]), T.ch[:, :], [b6, k_xs, k_yv])
+
+    remote([xfer(topo, core, me["helpers"][k], me["e_on"][k], T.sem.qc, T.xs[:, 2 * CAP * k:2 * CAP * (k + 1)], T.h1[:, :]) for k in range(2)], [b7])
+    remote([xfer(topo, core, cores[q], me["e_near"][j], T.sem.rc, T.xs[:, CAP * order.index(q):CAP * order.index(q) + CAP],
+                 T.cc[:, CAP * r:CAP * r + CAP]) for j, q in enumerate(near)], [b7])
+
+    k_zo = act(T.zo[:, :], T.dd[:, :], [k_dd], F.Copy, scale=4096.0)
+    k_idf = act(T.identf[:, :], T.ident[:, :], [k_id])
+    t_a = act(T.taba[:, :], T.fw[:, :].indirect(T.l0[:, :]), [w_id, w_fo, c_l0])
+    t_g0 = act(T.g0[:, :], T.st[:, 0:S].indirect(T.l0[:, :]), [l_st, c_l0])
+    m_t1 = wrap(T.p3[:, 0:128], T.zf, T.taba, B, [k_zf, t_a])
+    c_self = cp(T.cc[:, CAP * r:CAP * r + CAP], T.xs[:, W - CAP:W], [b7])
+    mine = T.st[:, VB + MISS * r:VB + MISS * (r + 1)]
+    k_mz = fill(mine, 0.0)
+    c_l1 = cp(T.l1[:, :], T.p3[:, 0:128], [m_t1])
+    t_b = cp(T.tabb[:, :], T.fw[:, :].indirect(T.l1[:, :]), [c_l1])
+    t_g1a = act(T.g1[:, 0:1536], T.st[:, 0:S].indirect(T.l1[:, 0:96]), [c_l1])
+    t_g1b = cp(T.g1[:, 1536:B], T.st[:, 0:S].indirect(T.l1[:, 96:128]), [c_l1, l_st])
+
+    k_jr = iota(T.jr[:, :], [[1, 64]], 0, 64, flt=False)
+    z0 = iota(T.zi[:, :], [[-S, 9], [0, 16]], 0, 0)
+    k_z1 = sel(T.z1[:, :], T.ones[:, 0:144], last, A.is_equal, 0.0, -3840, 1, [k_one])
+    z1 = sel(T.zi[:, :], T.zi[:, :], [[-16, 9], [0, 16]], A.not_equal, 1.0, -2, 1, [z0])
+    k_nw = sel(T.nw[:, :], T.nt[:, :], [[-1, 128]], A.not_equal, 8192.0, 0, 1, [k_nt])
+    z2 = sel(T.zi[:, :], T.zi[:, :], [[-16, 9], [0, 16]], A.not_equal, 1.0, -3, 1, [z1])
+    z3 = sel(T.zi[:, :], T.zi[:, :], last, A.is_ge, 0.0, -3842, 1, [z2])
+    k_zi = sel(T.zi[:, :], T.zi[:, :], upto, A.is_ge, 0.0, 4, -1, [z3])
+    k_yi = iota(T.yw[:, 0:VB], [[1, VB]], 0, 0)
+    j1 = ts(T.ja[:, :], T.jr[:, :], W - 1, A.bitwise_and, [k_jr])
+    k_z1f = act(T.z1f[:, :], T.z1[:, :], [k_z1])
+    k_ji = ts(T.ji[:, :], T.ja[:, :], float(S), A.add, [j1])
+    c_vf = cp(T.vf[:, :], T.vl[:, :], [l_va, x_v])
+    w_va = op("y", [(lambda q=q: Sy.dma_start(T.yw[0:128:16, VB + MISS * q:VB + MISS * (q + 1)], T.vf[:, 24 * q:24 * q + 24])) for q in range(N)],
+              [k_yv, c_vf], dma=True)
+
+    m_s2 = wrap(T.p0[:, 0:64], T.zw, T.cc, W, [x_c, c_self, b1])
+    e1 = ts(T.x2[:, :], T.p0[:, 0:64], 13.0, A.mult, [m_s2])
+    r1 = act(T.rr[:, :], T.p0[:, 0:64], [e1], F.Relu, scale=4096.0)
+    m_m0 = op("p", [mm(T.p3[:, 0:64], T.identf[:, :], T.ji[:, :], True, False), mm(T.p3[:, 0:64], T.identf[:, :], T.rr[:, :], False, True)],
+              [r1, k_ji, k_idf, c_l1], acc=True)
+    e2 = op("v", [lambda: V.tensor_scalar(T.ba[:, :], T.x2[:, :], 1, 0x7F0, A.arith_shift_right, A.bitwise_and),
+                  lambda: V.tensor_scalar(T.bb[:, :], T.x2[:, :], 12, 15, A.arith_shift_right, A.bitwise_and)], [e1])
+    e3 = tt(T.bc[:, :], T.ba[:, :], T.bb[:, :], A.add, [e2])
+    c_lb = cp(T.lb[:, :], T.bc[:, :], [e3])
+    s_tb = act(T.tbg[:, :], T.tabb[:, :].indirect(T.lb[:, :]), [c_lb, t_b])
+    n0 = tt(T.ne0[:, :], T.g0[:, :].indirect(T.lb[:, :]), T.cc[:, :], A.not_equal, [c_lb, t_g0])
+    s_m0 = act(T.m0[:, :], T.p3[:, 0:64], [m_m0])
+    n1a = tt(T.ne1[:, 0:512], T.g1[:, :].indirect(T.lb[:, 0:32]), T.cc[:, 0:512], A.not_equal, [c_lb, t_g1a, t_g1b])
+    m_l2 = wrap(T.p1[:, 0:64], T.zf, T.tbg, W, [s_tb, b5])
+    c_l2 = cp(T.l2[:, :], T.p1[:, 0:64], [m_l2])
+    n1b = tt(T.ne1[:, 512:W], T.g1[:, :].indirect(T.lb[:, 32:64]), T.cc[:, 512:W], A.not_equal, [c_lb])
+    wrap(T.p4[:, 0:64], T.zo, T.ne0, W, [n0, k_zo], stop=False)
+    wrap(T.p5[:, 0:64], T.zi, T.tbg, W, [k_zi], stop=False)
+    m_b1 = wrap(T.p5[:, 0:64], T.zo, T.ne1, W, [n1a, n1b], start=False)
+    s_t3 = act(T.t3g[:, :], T.fw[:, :].indirect(T.l2[:, :]), [c_l2])
+    n2 = tt(T.ne2[:, :], T.st[:, 0:S].indirect(T.l2[:, :]), T.cc[:, :], A.not_equal, [c_l2])
+    s_t2s = act(T.t2s[:, :], T.p1[:, 0:64], [c_l2])
+    s_ta = act(T.tag[:, :], T.taba[:, :].indirect(T.lb[:, :]), [c_lb, t_a])
+    m_l3 = wrap(T.p2[:, 0:64], T.zf, T.t3g, W, [s_t3, b6])
+    c_l3 = cp(T.l3[:, :], T.p2[:, 0:64], [m_l3])
+    n3 = tt(T.ne3[:, :], T.st[:, 0:S].indirect(T.l3[:, :]), T.cc[:, :], A.not_equal, [c_l3])
+    s_t3s = act(T.t3s[:, :], T.p2[:, 0:64], [c_l3])
+    m_b2 = wrap(T.p6[:, 0:64], T.zo, T.ne2, W, [n2, s_t2s, k_idf], start=False,
+                before=[mm(T.p6[:, 0:64], T.identf[:, :], T.t2s[:, :], True, False)])
+    m_b0 = wrap(T.p4[:, 0:64], T.zi, T.tag, W, [s_ta], start=False)
+    op("p", mm(T.p7[:, 0:64], T.identf[:, :], T.t3s[:, :], True, False), [s_t3s])
+    m_b3 = wrap(T.p7[:, 0:64], T.zo, T.ne3, W, [n3], start=False)
+    f2 = s_m0
+    for bank, m_b in ((T.p5, m_b1), (T.p6, m_b2), (T.p4, m_b0), (T.p7, m_b3)):
+        f2 = tt(T.mm[:, :], bank[:, 0:64], T.m0[:, :] if f2 == s_m0 else T.mm[:, :], A.min, [f2, m_b])
+
+    off = float(8193 - VB - MISS * r)
+    f3 = ts(T.ms[:, :], T.mm[:, :], 4096.0, A.is_ge, [f2])
+    f4 = scan(T.s2[:, :], T.ones[:, 0:64], T.ms[:, :], 0.0, A.subtract, [f3])
+    f5 = ts(T.mo[:, :], T.mm[:, :], 4096.0, A.min, [f2], off, A.add)
+    op("p", mm(T.p3[:, 0:64], T.nw[:, :], T.ms[:, :], True, False), [f3, k_nw, s_m0])
+    m_n = op("p", mm(T.p3[:, 0:64], T.nb[:, :], T.s2[:, :], False, True), [f4])
+    f6 = tt(T.uu[:, :], T.p3[:, 0:64], T.mo[:, :], A.max, [m_n, f5])
+    c_ix = ts(T.ix[:, :], T.uu[:, :], off, A.subtract, [f6])
+
+    wide = max(8 * (job[-1] - job[0] + 1) for job in me["jobs"][:2])
+    assert all(8 * job[0] + wide <= 64 for job in me["jobs"][:2])
+    remote([xfer(topo, core, me["helpers"][k], me["e_on"][k], T.sem.qa, T.ix[:, 8 * me["jobs"][k][0]:8 * me["jobs"][k][0] + wide],
+                 T.h2[:, 0:wide]) for k in range(2)], [c_ix])
+    remote([xfer(topo, core, cores[q], me["e_near"][j], T.sem.rn, T.ix[:, 8 * q:8 * q + 8],
+                 T.an[:, 8 * lay[q]["order"].index(r):8 * lay[q]["order"].index(r) + 8]) for j, q in enumerate(near)], [c_ix])
+
+    m_v = wrap(T.p0[:, 0:24], T.z1f, T.yw, MISS, [w_va, k_z1f, r1], a0=VB + MISS * r)
+    h1 = cp(T.st[:, :].indirect(T.ix[:, :]), T.cc[:, :], [c_ix, k_mz, n2, n3, t_g0, t_g1a, t_g1b])
+    c_lv = cp(T.lv[:, :], T.p0[:, 0:24], [m_v])
+    h2 = cp(T.st[:, 0:S].indirect(T.lv[:, :]), mine, [h1, c_lv])
+    o_z = dma("y", T.z[:, :], T.st[:, 0:S], [h2])
+
+    def block(b, lst):
+        return lambda: Sc.activation(T.ay[:, CAP * b:CAP * b + CAP], T.yw[:, :].indirect(lst), F.Identity, bias=float(S * order[b]))
+
+    def vblock(b, lst):
+        return lambda: V.tensor_scalar(T.ay[:, CAP * b:CAP * b + CAP], T.yw[:, :].indirect(lst), float(S * order[b]), None, A.add)
+    nf = len(far)
+    y0 = op("s", block(N - 1, T.ix[:, 8 * r:8 * r + 8]), [c_ix, w_va, k_yi])
+    y2 = op("s", [block(b, T.an[:, 8 * b:8 * b + 8]) for b in range(nf)], [x_f])
+    y3 = op("v", [vblock(b, T.an[:, 8 * b:8 * b + 8]) for b in range(nf, N - 1)], [x_n, w_va, k_yi])
+    y4 = act(T.yb[:, 0:384], T.ay[:, :].indirect(T.ld[:, 0:24]), [y0, y2, y3, b6])
+    y5 = cp(T.yb[:, 384:M], T.ay[:, :].indirect(T.ld[:, 24:48]), [y0, y2, y3, b6])
+    o_y = dma("s", T.y[:, :], T.yb[0:128:16, :], [y4, y5])
+    op("s", [], [o_y])
+    op("y", [], [o_z])
+    op("g", [], [x_l])
+    emit(ops, queues, T)

@@ -4,44 +4,51 @@ from concourse.mybir import AluOpType as A, ActivationFunctionType as F
 N, M, S, B, CAP, MISS = 8, 768, 3072, 2048, 128, 384
 W = N * CAP
 VB = S + W
-NCS, NDS = 60, 24
+R = S // 16
+BANK = 512
+FA, JV, HV, ZV = 2048, 104, 32, 38
+NCS, NDS = 70, 24
 
 SCRATCH = {
     "ch": ("sbuf", [128, M], "bfloat16"), "wc": ("sbuf", [128, 1], "float32"),
     "st": ("sbuf", [128, VB + N * MISS], "bfloat16"),
-    "hd": ("sbuf", [128, 128], "int32"), "fo": ("sbuf", [128, 192], "int32"), "va": ("sbuf", [128, 24], "int32"),
+    "hd": ("sbuf", [128, 152], "int32"), "fo": ("sbuf", [128, R], "int32"), "va": ("sbuf", [128, 24], "int32"),
     "ones": ("sbuf", [128, 256], "bfloat16"), "mones": ("sbuf", [128, 128], "bfloat16"),
     "xs": ("sbuf", [128, W], "bfloat16"), "fw": ("sbuf", [128, S], "bfloat16"), "rm": ("sbuf", [128, 384], "bfloat16"),
-    "d1": ("sbuf", [128, 144], "bfloat16"), "dd": ("sbuf", [128, 144], "bfloat16"), "zw": ("sbuf", [128, 144], "bfloat16"),
-    "zf": ("sbuf", [128, 144], "bfloat16"), "zi": ("sbuf", [128, 144], "bfloat16"), "zo": ("sbuf", [128, 144], "bfloat16"),
-    "z1": ("sbuf", [128, 144], "bfloat16"), "z1f": ("sbuf", [128, 144], "float32"),
-    "nb": ("sbuf", [128, 128], "bfloat16"), "nt": ("sbuf", [128, 128], "bfloat16"), "ntt": ("sbuf", [128, 128], "bfloat16"),
+    "dd": ("sbuf", [128, 144], "bfloat16"), "zw": ("sbuf", [128, 144], "bfloat16"),
+    "zf": ("sbuf", [128, 144], "bfloat16"), "za": ("sbuf", [128, 144], "bfloat16"), "zb": ("sbuf", [128, 144], "bfloat16"),
+    "pk": ("sbuf", [128, 144], "bfloat16"), "pj": ("sbuf", [128, 128], "bfloat16"),
+    "nb": ("sbuf", [128, 128], "bfloat16"), "nt": ("sbuf", [128, 128], "bfloat16"),
     "nw": ("sbuf", [128, 128], "bfloat16"),
     "ident": ("sbuf", [128, 128], "bfloat16"), "identf": ("sbuf", [128, 128], "float32"),
-    "kq": ("sbuf", [128, 384], "bfloat16"), "pcol": ("sbuf", [128, 1], "float32"),
-    "idhi": ("sbuf", [128, 256], "bfloat16"), "idlo": ("sbuf", [128, 256], "bfloat16"),
-    "fhb": ("sbuf", [128, 192], "bfloat16"), "flb": ("sbuf", [128, 192], "bfloat16"),
-    "l0": ("sbuf", [128, 128], "uint16"), "l1": ("sbuf", [128, 128], "uint16"),
+    "kq": ("sbuf", [128, 384], "bfloat16"),
+    "pi": ("sbuf", [128, 1], "int32"), "pr": ("sbuf", [128, 1], "float32"),
+    "pf": ("sbuf", [128, 1], "float32"), "pl": ("sbuf", [128, 1], "float32"),
+    "pa": ("sbuf", [128, 1], "float32"), "pb": ("sbuf", [128, 1], "float32"),
+    "idhi": ("sbuf", [128, R], "bfloat16"), "idlo": ("sbuf", [128, R], "bfloat16"), "idf": ("sbuf", [128, R], "float32"),
+    "fhb": ("sbuf", [128, R], "bfloat16"), "flb": ("sbuf", [128, R], "bfloat16"),
+    "hhb": ("sbuf", [128, 152], "bfloat16"), "hlb": ("sbuf", [128, 152], "bfloat16"),
+    "lf": ("sbuf", [128, R], "uint16"),
     "vf": ("sbuf", [128, 24 * N], "float32"), "vl": ("sbuf", [128, 24 * N], "int32"),
     "x1": ("sbuf", [128, 48], "int32"), "own": ("sbuf", [128, 48], "int32"),
     "mk": ("sbuf", [128, 384], "bfloat16"), "sm": ("sbuf", [128, 384], "bfloat16"), "dm": ("sbuf", [128, 384], "float16"),
     "ld": ("sbuf", [128, 48], "uint16"),
     "cc": ("sbuf", [128, W], "bfloat16"),
-    "taba": ("sbuf", [128, B], "bfloat16"), "tabb": ("sbuf", [128, B], "bfloat16"),
-    "g0": ("sbuf", [128, B], "bfloat16"), "g1": ("sbuf", [128, B], "bfloat16"),
-    "jr": ("sbuf", [128, 64], "int32"), "ja": ("sbuf", [128, 64], "int32"), "ji": ("sbuf", [128, 64], "float32"),
-    "x2": ("sbuf", [128, 64], "int32"), "ba": ("sbuf", [128, 64], "int32"), "bb": ("sbuf", [128, 64], "int32"),
-    "bc": ("sbuf", [128, 64], "int32"), "lb": ("sbuf", [128, 64], "uint16"),
-    "l2": ("sbuf", [128, 64], "uint16"), "l3": ("sbuf", [128, 64], "uint16"),
-    "tag": ("sbuf", [128, W], "bfloat16"), "tbg": ("sbuf", [128, W], "bfloat16"), "t3g": ("sbuf", [128, W], "bfloat16"),
-    "ne0": ("sbuf", [128, W], "bfloat16"), "ne1": ("sbuf", [128, W], "bfloat16"),
-    "ne2": ("sbuf", [128, W], "bfloat16"), "ne3": ("sbuf", [128, W], "bfloat16"),
-    "t2s": ("sbuf", [128, 64], "float32"), "t3s": ("sbuf", [128, 64], "float32"),
+    "gs": ("sbuf", [128, S], "bfloat16"), "gj": ("sbuf", [128, S], "bfloat16"),
+    "ji": ("sbuf", [128, 64], "float32"),
+    "x2": ("sbuf", [128, 64], "int32"), "ba": ("sbuf", [128, 64], "int32"), "lb": ("sbuf", [128, 64], "uint16"),
+    "l0": ("sbuf", [128, 64], "uint16"), "l2": ("sbuf", [128, 64], "uint16"),
+    "l0f": ("sbuf", [128, 64], "float32"), "l2f": ("sbuf", [128, 64], "float32"),
+    "hg": ("sbuf", [128, W], "bfloat16"),
+    "da": ("sbuf", [128, W], "bfloat16"), "db": ("sbuf", [128, W], "bfloat16"),
+    "aa": ("sbuf", [128, W], "bfloat16"), "ab": ("sbuf", [128, W], "bfloat16"),
     "mm": ("sbuf", [128, 64], "float32"), "rr": ("sbuf", [128, 64], "float32"), "m0": ("sbuf", [128, 64], "float32"),
     "mo": ("sbuf", [128, 64], "float32"), "uu": ("sbuf", [128, 64], "float32"),
     "ms": ("sbuf", [128, 64], "bfloat16"), "s2": ("sbuf", [128, 64], "bfloat16"),
     "ix": ("sbuf", [128, 64], "uint16"), "lv": ("sbuf", [128, 24], "uint16"), "an": ("sbuf", [128, 64], "uint16"),
     "yw": ("sbuf", [128, VB + N * MISS], "float32"),
+    "sw": ("sbuf", [128, VB + N * MISS], "float32"), "cf": ("sbuf", [128, W - 16 * ZV], "float32"), "sb": ("sbuf", [128, MISS], "bfloat16"),
+    "mp": ("sbuf", [128, 64], "float32"), "mq": ("sbuf", [128, 64], "float32"),
     "ay": ("sbuf", [128, W], "float32"), "yb": ("sbuf", [128, M], "float32"),
     "h1": ("sbuf", [128, 2 * CAP], "bfloat16"), "h2": ("sbuf", [128, 64], "uint16"),
     "p0": ("psum", [128, 512], "float32"), "p1": ("psum", [128, 512], "float32"),
@@ -77,12 +84,16 @@ def layout(cores, r, topo):
     cand = sorted([h for h in topo.cores_of(c) if h not in cores], key=lambda h: (topo.die(h) != topo.die(c), h))
     helpers = [h for h in cand if all(topo.may_write(h, cores[q]) for q in far)][:2]
     helpers.append([h for h in cand if h not in helpers and all(topo.may_write(h, cores[q]) for q in near)][0])
-    on = topo.engines(c, helpers[0])
+    on, off = topo.engines(c, helpers[0]), topo.engines(c, cores[near[0]])
     half = len(far) // 2
-    jobs = [far[:half], far[half:], near]
-    return {"near": near, "far": far, "helpers": helpers, "jobs": jobs, "order": far + near + [r],
-            "e_near": share(topo.engines(c, cores[near[0]]), len(near)), "e_on": share(on, 2), "e_vac": share(on, 3),
-            "e_help": [share(topo.engines(helpers[k], cores[jobs[k][0]]), len(jobs[k])) for k in range(3)]}
+    third = min(near, key=lambda q: (q - r) % N)
+    direct = [q for q in near if q != third]
+    jobs = [far[:half], far[half:], [third]]
+    vjobs = [far[:half], far[half:], near]
+    return {"near": near, "far": far, "direct": direct, "helpers": helpers, "jobs": jobs, "vjobs": vjobs, "order": far + near + [r],
+            "e_direct": share(off, len(direct)), "e_feed": share(on, 2) + [[e for e in on if e not in off]], "e_vac": share(on, 3),
+            "e_help": [share(topo.engines(helpers[k], cores[jobs[k][0]]), len(jobs[k])) for k in range(3)],
+            "e_vhelp": [share(topo.engines(helpers[k], cores[vjobs[k][0]]), len(vjobs[k])) for k in range(3)]}
 
 
 def xfer(topo, src_core, dst_core, engines, sem, src, dst):
@@ -94,12 +105,9 @@ def helper_program(g, core, T, topo, lay, r, k):
     cores, me = T.cores, lay[r]
     job, eng = me["jobs"][k], me["e_help"][k]
     g.wait_ge(T.sem.qv, len(me["e_vac"][k]))
-    g.remote_dma_fused([xfer(topo, core, cores[q], eng[j], T.sem.rv, T.va[:, :], T.vl[:, 24 * r:24 * r + 24])
-                        for j, q in enumerate(job)], local_sem=T.sem.ls)
-    if k == 2:
-        g.wait_ge(T.sem.ls, sum(len(e) for e in eng))
-        return
-    got = len(me["e_on"][k])
+    g.remote_dma_fused([xfer(topo, core, cores[q], me["e_vhelp"][k][j], T.sem.rv, T.va[:, :], T.vl[:, 24 * r:24 * r + 24])
+                        for j, q in enumerate(me["vjobs"][k])], local_sem=T.sem.ls)
+    got = len(me["e_feed"][k])
     g.wait_ge(T.sem.qc, got)
     g.remote_dma_fused([xfer(topo, core, cores[q], eng[j], T.sem.rc, T.h1[:, CAP * j:CAP * j + CAP], T.cc[:, CAP * r:CAP * r + CAP])
                         for j, q in enumerate(job)], local_sem=T.sem.ls)
@@ -109,7 +117,7 @@ def helper_program(g, core, T, topo, lay, r, k):
         a, b = 8 * (q - job[0]), 8 * lay[q]["order"].index(r)
         tr.append(xfer(topo, core, cores[q], eng[j], T.sem.rf, T.h2[:, a:a + 8], T.an[:, b:b + 8]))
     g.remote_dma_fused(tr, local_sem=T.sem.ls)
-    g.wait_ge(T.sem.ls, 3 * sum(len(e) for e in eng))
+    g.wait_ge(T.sem.ls, 2 * sum(len(e) for e in eng) + sum(len(e) for e in me["e_vhelp"][k]))
 
 
 def emit(ops, queues, T):
@@ -165,7 +173,7 @@ def rank_program(g, core, T, topo):
                 helper_program(g, core, T, topo, lay, q, lay[q]["helpers"].index(core))
         return
     me = lay[r]
-    order, near, far = me["order"], me["near"], me["far"]
+    order, near, far, direct = me["order"], me["near"], me["far"], me["direct"]
     V, Sc, PE, Sy = g.vector, g.scalar, g.tensor, g.sync
     queues = {"g": g, "v": V, "s": Sc, "p": PE, "y": Sy, None: None}
     ops = []
@@ -180,6 +188,9 @@ def rank_program(g, core, T, topo):
 
     def dma(q, out, in_, deps=()):
         return op(q, lambda: queues[q].dma_start(out, in_), deps, dma=True)
+
+    def dmas(q, pairs, deps=()):
+        return op(q, [(lambda o=o, i=i: queues[q].dma_start(o, i)) for o, i in pairs], deps, dma=True)
 
     def ts(out, in0, s1, op0, deps, s2=None, op1=None):
         if op1 is None:
@@ -201,13 +212,14 @@ def rank_program(g, core, T, topo):
     def act(out, in_, deps, func=F.Copy, **kw):
         return op("s", lambda: Sc.activation(out, in_, func, **kw), deps)
 
+    def move(q, out, in_, deps):
+        return cp(out, in_, deps) if q == "v" else act(out, in_, deps)
+
     def sel(out, in_, pattern, cmp, fillv, base, cm, deps):
         return op("g", lambda: g.affine_select(out, in_, pattern, cmp, fillv, base, cm), deps)
 
-    def iota(out, pattern, base, cm, deps=(), flt=True):
-        if flt:
-            return op("g", lambda: g.iota(out, pattern, base, cm, allow_small_or_imprecise_dtypes=True), deps)
-        return op("g", lambda: g.iota(out, pattern, base, cm), deps)
+    def iota(out, pattern, base, cm):
+        return op("g", lambda: g.iota(out, pattern, base, cm, allow_small_or_imprecise_dtypes=True))
 
     def mm(out, lhsT, rhs, start, stop):
         return lambda: PE.matmul(out, lhsT, rhs, start, stop)
@@ -219,140 +231,181 @@ def rank_program(g, core, T, topo):
     def remote(transfers, deps):
         return op("g", lambda: g.remote_dma_fused(transfers, local_sem=T.sem.ls), deps)
 
-    def landing(key, k, senders):
-        return sum(len(lay[q][key][k][lay[q]["jobs"][k].index(r)]) for q in senders if r in lay[q]["jobs"][k])
+    def landing(key, jobs):
+        return sum(len(lay[q][key][k][lay[q][jobs][k].index(r)]) for q in range(N) for k in range(3) if r in lay[q][jobs][k])
 
-    n_near = sum(len(lay[q]["e_near"][lay[q]["near"].index(r)]) for q in near)
-    n_far = landing("e_help", 0, far) + landing("e_help", 1, far)
-    x_v = ext("rv", n_far + landing("e_help", 2, near))
+    n_near = sum(len(lay[q]["e_direct"][lay[q]["direct"].index(r)]) for q in near if r in lay[q]["direct"])
+    n_far = landing("e_help", "jobs")
+    x_v = ext("rv", landing("e_vhelp", "vjobs"))
     x_c, x_n, x_f = ext("rc", n_near + n_far), ext("rn", n_near), ext("rf", n_far)
-    x_l = ext("ls", sum(len(e) for e in me["e_vac"]) + 2 * (sum(len(e) for e in me["e_near"]) + sum(len(e) for e in me["e_on"])))
+    x_l = ext("ls", sum(len(e) for e in me["e_vac"]) + 2 * (sum(len(e) for e in me["e_direct"]) + sum(len(e) for e in me["e_feed"])))
 
-    l_va = dma("y", T.vl[:, 24 * r:24 * r + 24], T.vac[:, :])
-    l_wt = dma("s", T.wc[:, :], T.wt[:, :])
+    l_wt = dma("y", T.wc[:, :], T.wt[:, :])
+    l_va = dma("s", T.vl[:, 24 * r:24 * r + 24], T.vac[:, :])
     l_ch = dma("y", T.ch[:, :], T.chunks[:, :])
-    l_fo = dma("s", T.fo[:, :], T.follow[:, :])
-    l_hd = dma("s", T.hd[:, :], T.head[:, :])
+    l_fo = dma("y", T.fo[:, :], T.follow[:, :])
+    l_st = dma("y", T.st[:, 0:S], T.store[:, :])
+    l_hd = dmas("y", [(T.hd[:, 0:128], T.head[:, :]), (T.hd[:, 128:152], T.vac[:, :])])
 
-    k_one = fill(T.ones[:, :], 1.0)
+    upto, from_ = [[16, 9], [0, 16]], [[-16, 9], [0, 16]]
+    k_p = iota(T.pf[:, :], [[0, 1]], 0, 1)
     k_mon = fill(T.mones[:, :], -1.0)
-    k_idlo = scan(T.idlo[:, :], T.ones[:, :], T.ones[:, :], -1.0, A.add, [k_one])
-    k_rm0 = fill(T.rm[:, :], 1.0)
-    k_fw = fill(T.fw[:, :], 1.0)
-    k_rm = fill(T.rm[:, 0:384:48], 0.0, [k_rm0])
-    last = [[-16, 9], [256, 16]]
-    upto = [[16, 9], [0, 16]]
-    k_pc = iota(T.pcol[:, :], [[0, 1]], 0, 256)
-    k_d1 = sel(T.d1[:, :], T.ones[:, 0:144], last, A.is_ge, 0.0, -3840, 1, [k_one])
+    k_one = fill(T.ones[:, :], 1.0)
+    k_gi = ts(T.pi[:, :], T.pf[:, :], 0.0625, A.mult, [k_p], -0.46875, A.add)
+    k_idlo = scan(T.idlo[:, :], T.ones[:, 0:R], T.ones[:, 0:R], -1.0, A.add, [k_one])
+    k_pl = ts(T.pl[:, :], T.pi[:, :], 16.0, A.mult, [k_gi], 15.0, A.add)
+    k_pk0 = fill(T.pk[:, :], 0.0)
+    k_fwa = fill(T.fw[:, 0:FA], 0.0)
     k_nt0 = sel(T.nt[:, :], T.mones[:, :], [[-1, 128]], A.is_ge, 0.0, 0, 1, [k_mon])
-    k_dd = sel(T.dd[:, :], T.d1[:, :], upto, A.is_ge, 0.0, 15, -1, [k_d1])
+    k_nb0 = sel(T.nb[:, :], T.mones[:, :], [[-16, 8], [0, 16]], A.is_ge, 0.0, 0, 1, [k_mon])
     k_nt = sel(T.nt[:, :], T.nt[:, :], [[16, 8], [0, 16]], A.is_ge, 0.0, 15, -1, [k_nt0])
-    k_idhi = act(T.idhi[:, :], T.ones[:, :], [k_one, k_pc], F.Identity, bias=T.pcol[:, :], scale=0.0)
+    k_nb = sel(T.nb[:, :], T.nb[:, :], [[16, 8], [0, 16]], A.is_ge, 0.0, 15, -1, [k_nb0])
     k_xs = op("s", [(lambda a=a: Sc.activation(T.xs[:, a:a + 256], T.ones[:, :], F.Copy, scale=-1.0)) for a in range(0, W, 256)], [k_one])
+    k_pr = act(T.pr[:, :], T.pl[:, :], [k_pl], F.Identity, bias=T.pf[:, :], scale=-1.0)
     k_kq = op("s", [(lambda b=b: Sc.activation(T.kq[:, 48 * b:48 * b + 48], T.ones[:, 0:48], F.Copy, scale=-8.0 * b)) for b in range(N)], [k_one])
-    k_yv = op("s", [(lambda a=a: Sc.activation(T.yw[:, VB + a:VB + a + W], T.xs[:, :], F.Copy)) for a in range(0, N * MISS, W)], [k_xs])
-    k_ntt = op("v", lambda: V.transpose(T.ntt[:, :], T.nt[:, :]), [k_nt])
-    k_zw = ts(T.zw[:, :], T.dd[:, :], T.wc[:, :], A.mult, [k_dd, l_wt])
-    k_nb = tt(T.nb[:, :], T.nt[:, :], T.ntt[:, :], A.min, [k_ntt])
-    k_id = tt(T.ident[:, :], T.nt[:, :], T.ntt[:, :], A.mult, [k_ntt])
+    k_pa = act(T.pa[:, :], T.pr[:, :], [k_pr], F.Identity, bias=15.0 * R, scale=float(R))
+    k_pb = act(T.pb[:, :], T.pr[:, :], [k_pr], F.Identity, bias=15.0 * 64 + S, scale=64.0)
+    k_idhi = act(T.idhi[:, :], T.ones[:, 0:R], [k_pa], F.Identity, bias=T.pa[:, :], scale=0.0)
+    mine, mine_s = T.st[:, VB + MISS * r:VB + MISS * (r + 1)], T.sw[:, VB + MISS * r:VB + MISS * (r + 1)]
+    k_sz = act(mine_s, T.xs[:, 0:MISS], [k_xs], F.Silu, scale=0.0)
+    k_zw = ts(T.zw[:, :], T.idlo[:, 0:144], T.pl[:, :], A.is_equal, [k_idlo, k_pl, l_wt], T.wc[:, :], A.mult)
+    k_rm0 = fill(T.rm[:, :], 1.0)
+    k_fw = fill(T.fw[:, FA:S], 0.0)
 
     remote([xfer(topo, core, me["helpers"][k], me["e_vac"][k], T.sem.qv, T.vl[:, 24 * r:24 * r + 24], T.va[:, :]) for k in range(3)], [l_va])
-    k_zf = sel(T.zf[:, :], T.d1[:, :], upto, A.is_ge, 0.0, 1, -1, [k_d1])
+    k_pk = k_pk0
+    for k in range(3):
+        k_pk = sel(T.pk[:, :], T.pk[:, :], [[-16, 9], [-3, 16]], A.not_equal, 4096.0 * 256 ** k, 30 - k, 1, [k_pk])
+    k_pk = sel(T.pk[:, :], T.pk[:, :], upto, A.is_ge, 0.0, 15, -1, [k_pk])
+    k_pk = sel(T.pk[:, :], T.pk[:, :], from_, A.is_ge, 0.0, 0, 1, [k_pk])
+    pk_a, pk_b = T.pk[:, 0:128], T.pk[:, 6:134]
 
-    a1 = cp(T.fhb[:, :], T.fo[:, :], [l_fo])
-    w_id = op("y", [lambda: Sy.dma_start(T.fw[3:128:16, :], T.idlo[0:96, :]), lambda: Sy.dma_start(T.fw[2:128:16, :], T.idhi[0:96, :])],
-              [k_fw, k_idlo, k_idhi], dma=True)
     m_s1 = wrap(T.p0[:, 0:48], T.zw, T.ch, M, [k_zw, l_ch])
-    a2 = tt(T.flb[:, :], T.fo[:, :], T.fhb[:, :], A.subtract, [a1])
-    w_fo = op("y", [lambda: Sy.dma_start(T.fw[0:128:16, :], T.fhb[:, :]), lambda: Sy.dma_start(T.fw[1:128:16, :], T.flb[:, :])],
-              [k_fw, a1, a2], dma=True)
-    l_st = dma("y", T.st[:, 0:S], T.store[:, :])
     b1 = ts(T.x1[:, :], T.p0[:, 0:48], 13.0, A.mult, [m_s1])
+    k_rm = fill(T.rm[:, 0:384:48], 0.0, [k_rm0])
     b2 = ts(T.own[:, :], T.x1[:, :], 2, A.arith_shift_right, [b1], 7, A.bitwise_and)
+    k_id = ts(T.ident[:, :], T.idlo[:, 0:128], T.pf[:, :], A.is_equal, [k_idlo])
     b3 = op("v", [(lambda b=b: V.tensor_scalar(T.mk[:, 48 * b:48 * b + 48], T.own[:, :], float(order[b]), None, A.is_equal)) for b in range(N)], [b2])
     b4 = scan(T.sm[:, :], T.rm[:, :], T.mk[:, :], 0.0, A.subtract, [b3, k_rm])
-    c_l0 = cp(T.l0[:, :], T.hd[:, :], [l_hd])
-    op("p", mm(T.p1[:, 0:384], T.nb[:, :], T.kq[:, :], True, False), [k_nb, k_kq])
-    op("p", mm(T.p1[:, 0:384], T.nt[:, :], T.mk[:, :], False, False), [k_nt, b3])
+    c_lf = cp(T.lf[:, :], T.fo[:, :], [l_fo])
+    op("p", mm(T.p1[:, 0:384], T.nt[:, :], T.mk[:, :], True, False), [k_nt, b3])
+    op("p", mm(T.p1[:, 0:384], T.nb[:, :], T.kq[:, :], False, False), [k_nb, k_kq])
     m_pos = op("p", mm(T.p1[:, 0:384], T.nb[:, :], T.sm[:, :], False, True), [b4])
+    a1 = cp(T.fhb[:, :], T.fo[:, :], [l_fo])
     b5 = tt(T.dm[:, :], T.p1[:, 0:384], T.mk[:, :], A.mult, [m_pos])
-    m_de = op("p", [mm(T.p2[:, 0:48], T.ident[:, :], T.dm[:, 48 * b:48 * b + 48], b == 0, b == N - 1) for b in range(N)], [b5, k_id], acc=True)
-    b6 = cp(T.ld[:, :], T.p2[:, 0:48], [m_de])
-    b7 = cp(T.xs[:, :].indirect(T.ld[:, :]), T.ch[:, :], [b6, k_xs, k_yv])
+    m_de = op("p", [mm(T.p0[:, 0:48], T.ident[:, :], T.dm[:, 48 * b:48 * b + 48], b == 0, b == N - 1) for b in range(N)], [b5, k_id, b1], acc=True)
+    a2 = tt(T.flb[:, :], T.fo[:, :], T.fhb[:, :], A.subtract, [a1])
+    w_fo = dmas("y", [(T.fw[3:128:16, :], T.idlo[:, :]), (T.fw[2:128:16, :], T.idhi[:, :]),
+                      (T.fw[0:128:16, :], T.fhb[:, :]), (T.fw[1:128:16, :], T.flb[:, :])], [k_fwa, k_fw, k_idlo, k_idhi, a1, a2])
+    b6 = cp(T.ld[:, :], T.p0[:, 0:48], [m_de])
+    b7 = cp(T.xs[:, :].indirect(T.ld[:, :]), T.ch[:, :], [b6, k_xs, k_sz])
 
-    remote([xfer(topo, core, me["helpers"][k], me["e_on"][k], T.sem.qc, T.xs[:, 2 * CAP * k:2 * CAP * (k + 1)], T.h1[:, :]) for k in range(2)], [b7])
-    remote([xfer(topo, core, cores[q], me["e_near"][j], T.sem.rc, T.xs[:, CAP * order.index(q):CAP * order.index(q) + CAP],
-                 T.cc[:, CAP * r:CAP * r + CAP]) for j, q in enumerate(near)], [b7])
+    def blk(q):
+        return T.xs[:, CAP * order.index(q):CAP * order.index(q) + CAP]
+    third = me["jobs"][2][0]
+    remote([xfer(topo, core, me["helpers"][k], me["e_feed"][k], T.sem.qc, T.xs[:, 2 * CAP * k:2 * CAP * (k + 1)], T.h1[:, :]) for k in range(2)], [b7])
+    remote([xfer(topo, core, cores[q], me["e_direct"][j], T.sem.rc, blk(q), T.cc[:, CAP * r:CAP * r + CAP]) for j, q in enumerate(direct)]
+           + [xfer(topo, core, me["helpers"][2], me["e_feed"][2], T.sem.qc, blk(third), T.h1[:, 0:CAP])], [b7])
 
-    k_zo = act(T.zo[:, :], T.dd[:, :], [k_dd], F.Copy, scale=4096.0)
-    k_idf = act(T.identf[:, :], T.ident[:, :], [k_id])
-    t_a = act(T.taba[:, :], T.fw[:, :].indirect(T.l0[:, :]), [w_id, w_fo, c_l0])
-    t_g0 = act(T.g0[:, :], T.st[:, 0:S].indirect(T.l0[:, :]), [l_st, c_l0])
-    m_t1 = wrap(T.p3[:, 0:128], T.zf, T.taba, B, [k_zf, t_a])
+    banks = [T.p2, T.p3, T.p4, T.p5, T.p6, T.p7]
+    t_g = act(T.gs[:, :], T.st[:, 0:S].indirect(T.lf[:, :]), [l_st, c_lf])
     c_self = cp(T.cc[:, CAP * r:CAP * r + CAP], T.xs[:, W - CAP:W], [b7])
-    mine = T.st[:, VB + MISS * r:VB + MISS * (r + 1)]
-    k_mz = fill(mine, 0.0)
-    c_l1 = cp(T.l1[:, :], T.p3[:, 0:128], [m_t1])
-    t_b = cp(T.tabb[:, :], T.fw[:, :].indirect(T.l1[:, :]), [c_l1])
-    t_g1a = act(T.g1[:, 0:1536], T.st[:, 0:S].indirect(T.l1[:, 0:96]), [c_l1])
-    t_g1b = cp(T.g1[:, 1536:B], T.st[:, 0:S].indirect(T.l1[:, 96:128]), [c_l1, l_st])
+    k_dd = ts(T.dd[:, :], T.idlo[:, 0:144], T.pl[:, :], A.is_equal, [])
+    a3 = cp(T.hhb[:, :], T.hd[:, :], [l_hd])
+    t_jv = cp(T.gj[:, 0:16 * JV], T.fw[:, :].indirect(T.lf[:, 0:JV]), [w_fo, c_lf])
+    t_js = act(T.gj[:, 16 * JV:S], T.fw[:, :].indirect(T.lf[:, JV:R]), [w_fo, c_lf])
+    a4 = tt(T.hlb[:, :], T.hd[:, :], T.hhb[:, :], A.subtract, [a3])
+    w_hd = dmas("y", [(T.fw[10:128:16, 0:B], T.hhb[:, 0:128]), (T.fw[11:128:16, 0:B], T.hlb[:, 0:128]),
+                      (T.fw[10:128:16, B:B + MISS], T.hhb[:, 128:152]), (T.fw[11:128:16, B:B + MISS], T.hlb[:, 128:152])], [a3, a4, t_jv, t_js])
+    k_pj = sel(T.pj[:, :], T.ident[:, :], [[16, 8], [0, 16]], A.is_ge, 0.0, 3, -1, [k_id])
 
-    k_jr = iota(T.jr[:, :], [[1, 64]], 0, 64, flt=False)
-    z0 = iota(T.zi[:, :], [[-S, 9], [0, 16]], 0, 0)
-    k_z1 = sel(T.z1[:, :], T.ones[:, 0:144], last, A.is_equal, 0.0, -3840, 1, [k_one])
-    z1 = sel(T.zi[:, :], T.zi[:, :], [[-16, 9], [0, 16]], A.not_equal, 1.0, -2, 1, [z0])
+    def unperm(k, lhsT, src, stop):
+        fns, a = [], BANK * k
+        while a < BANK * (k + 1):
+            i, c0 = divmod(a, R)
+            n = min(R - c0, BANK * (k + 1) - a)
+            fns.append((banks[k][:, a - BANK * k:a - BANK * k + n], src[:, 16 * c0 + i:16 * (c0 + n - 1) + i + 1:16]))
+            a += n
+        return [mm(o, lhsT, s, False, stop and j == len(fns) - 1) for j, (o, s) in enumerate(fns)]
+    op("p", [mm(banks[k][:, :], pk_a, T.st[:, BANK * k:BANK * (k + 1)], True, False) for k in range(6)], [k_pk, l_st], acc=True)
+    op("p", [f for k in range(6) for f in unperm(k, pk_b, T.gs, False)], [t_g], acc=True)
+    m_u = [op("p", unperm(k, T.pj[:, :], T.gj, True), [t_jv, t_js, k_pj], acc=True) for k in range(6)]
+    c_u = [move("vs"[k % 2], T.yw[:, BANK * k:BANK * (k + 1)], banks[k][:, :], [m_u[k]]) for k in range(6)]
+
+    k_za = sel(T.za[:, :], T.dd[:, :], from_, A.is_ge, 0.0, -10, 1, [k_dd])
+    k_zf = sel(T.zf[:, :], T.dd[:, :], upto, A.is_ge, 0.0, 1, -1, [k_dd])
+    k_zb0 = sel(T.zb[:, :], T.dd[:, :], upto, A.is_ge, 0.0, 9, -1, [k_dd])
     k_nw = sel(T.nw[:, :], T.nt[:, :], [[-1, 128]], A.not_equal, 8192.0, 0, 1, [k_nt])
-    z2 = sel(T.zi[:, :], T.zi[:, :], [[-16, 9], [0, 16]], A.not_equal, 1.0, -3, 1, [z1])
-    z3 = sel(T.zi[:, :], T.zi[:, :], last, A.is_ge, 0.0, -3842, 1, [z2])
-    k_zi = sel(T.zi[:, :], T.zi[:, :], upto, A.is_ge, 0.0, 4, -1, [z3])
-    k_yi = iota(T.yw[:, 0:VB], [[1, VB]], 0, 0)
-    j1 = ts(T.ja[:, :], T.jr[:, :], W - 1, A.bitwise_and, [k_jr])
-    k_z1f = act(T.z1f[:, :], T.z1[:, :], [k_z1])
-    k_ji = ts(T.ji[:, :], T.ja[:, :], float(S), A.add, [j1])
-    c_vf = cp(T.vf[:, :], T.vl[:, :], [l_va, x_v])
-    w_va = op("y", [(lambda q=q: Sy.dma_start(T.yw[0:128:16, VB + MISS * q:VB + MISS * (q + 1)], T.vf[:, 24 * q:24 * q + 24])) for q in range(N)],
-              [k_yv, c_vf], dma=True)
+    k_zb = sel(T.zb[:, :], T.zb[:, :], from_, A.is_ge, 0.0, -2, 1, [k_zb0])
+    k_yv = op("g", [(lambda a=a: g.iota(T.yw[:, VB + a:VB + a + W], [[0, W]], 0, 0, allow_small_or_imprecise_dtypes=True)) for a in range(0, N * MISS, W)])
+    k_idf = act(T.identf[:, :], T.ident[:, :], [k_id])
+    k_ji = act(T.ji[:, :], T.idlo[:, 0:64], [k_idlo, k_pb], F.Identity, bias=T.pb[:, :])
 
-    m_s2 = wrap(T.p0[:, 0:64], T.zw, T.cc, W, [x_c, c_self, b1])
+    H = W // 2
+    U = T.yw[:, 0:S]
+    m_s2 = wrap(T.p0[:, 0:64], T.zw, T.cc, W, [x_c, c_self, b6])
+    m_pk = [op("p", [mm(bank[:, :], pk_a, T.cc[:, H * h:H * (h + 1)], True, False), mm(bank[:, :], pk_b, T.cc[:, H * h:H * (h + 1)], False, True)],
+               [b5, c_u[0]], acc=True) for h, bank in enumerate((T.p1, T.p2))]
     e1 = ts(T.x2[:, :], T.p0[:, 0:64], 13.0, A.mult, [m_s2])
     r1 = act(T.rr[:, :], T.p0[:, 0:64], [e1], F.Relu, scale=4096.0)
+    e2 = ts(T.ba[:, :], T.x2[:, :], 5, A.arith_shift_right, [e1], B - 1, A.bitwise_and)
+    c_lb = cp(T.lb[:, :], T.ba[:, :], [e2])
+    s_hv = cp(T.hg[:, 0:16 * HV], T.fw[:, 0:B].indirect(T.lb[:, 0:HV]), [c_lb, w_hd])
+    s_hs = act(T.hg[:, 16 * HV:W], T.fw[:, 0:B].indirect(T.lb[:, HV:64]), [c_lb, w_hd])
     m_m0 = op("p", [mm(T.p3[:, 0:64], T.identf[:, :], T.ji[:, :], True, False), mm(T.p3[:, 0:64], T.identf[:, :], T.rr[:, :], False, True)],
-              [r1, k_ji, k_idf, c_l1], acc=True)
-    e2 = op("v", [lambda: V.tensor_scalar(T.ba[:, :], T.x2[:, :], 1, 0x7F0, A.arith_shift_right, A.bitwise_and),
-                  lambda: V.tensor_scalar(T.bb[:, :], T.x2[:, :], 12, 15, A.arith_shift_right, A.bitwise_and)], [e1])
-    e3 = tt(T.bc[:, :], T.ba[:, :], T.bb[:, :], A.add, [e2])
-    c_lb = cp(T.lb[:, :], T.bc[:, :], [e3])
-    s_tb = act(T.tbg[:, :], T.tabb[:, :].indirect(T.lb[:, :]), [c_lb, t_b])
-    n0 = tt(T.ne0[:, :], T.g0[:, :].indirect(T.lb[:, :]), T.cc[:, :], A.not_equal, [c_lb, t_g0])
+              [r1, k_ji, k_idf, c_u[1]], acc=True)
+    m_l0 = wrap(T.p4[:, 0:64], T.za, T.hg, W, [s_hv, s_hs, k_za, c_u[2]])
+    c_pk0 = act(T.yw[:, S:S + H], T.p1[:, :], [m_pk[0]])
+    c_pk1 = act(T.yw[:, S + H:S + W], T.p2[:, :], [m_pk[1]])
+    k_mz = fill(mine, 0.0)
+    c_vf = cp(T.vf[:, :], T.vl[:, :], [l_va, x_v])
+    w_va = dmas("y", [(T.yw[0:128:16, VB + MISS * q:VB + MISS * (q + 1)], T.vf[:, 24 * q:24 * q + 24]) for q in range(N)], [k_yv, c_vf])
+    c_l0 = cp(T.l0[:, :], T.p4[:, 0:64], [m_l0])
+    s_l0 = act(T.l0f[:, :], T.p4[:, 0:64], [c_l0])
     s_m0 = act(T.m0[:, :], T.p3[:, 0:64], [m_m0])
-    n1a = tt(T.ne1[:, 0:512], T.g1[:, :].indirect(T.lb[:, 0:32]), T.cc[:, 0:512], A.not_equal, [c_lb, t_g1a, t_g1b])
-    m_l2 = wrap(T.p1[:, 0:64], T.zf, T.tbg, W, [s_tb, b5])
-    c_l2 = cp(T.l2[:, :], T.p1[:, 0:64], [m_l2])
-    n1b = tt(T.ne1[:, 512:W], T.g1[:, :].indirect(T.lb[:, 32:64]), T.cc[:, 512:W], A.not_equal, [c_lb])
-    wrap(T.p4[:, 0:64], T.zo, T.ne0, W, [n0, k_zo], stop=False)
-    wrap(T.p5[:, 0:64], T.zi, T.tbg, W, [k_zi], stop=False)
-    m_b1 = wrap(T.p5[:, 0:64], T.zo, T.ne1, W, [n1a, n1b], start=False)
-    s_t3 = act(T.t3g[:, :], T.fw[:, :].indirect(T.l2[:, :]), [c_l2])
-    n2 = tt(T.ne2[:, :], T.st[:, 0:S].indirect(T.l2[:, :]), T.cc[:, :], A.not_equal, [c_l2])
-    s_t2s = act(T.t2s[:, :], T.p1[:, 0:64], [c_l2])
-    s_ta = act(T.tag[:, :], T.taba[:, :].indirect(T.lb[:, :]), [c_lb, t_a])
-    m_l3 = wrap(T.p2[:, 0:64], T.zf, T.t3g, W, [s_t3, b6])
-    c_l3 = cp(T.l3[:, :], T.p2[:, 0:64], [m_l3])
-    n3 = tt(T.ne3[:, :], T.st[:, 0:S].indirect(T.l3[:, :]), T.cc[:, :], A.not_equal, [c_l3])
-    s_t3s = act(T.t3s[:, :], T.p2[:, 0:64], [c_l3])
-    m_b2 = wrap(T.p6[:, 0:64], T.zo, T.ne2, W, [n2, s_t2s, k_idf], start=False,
-                before=[mm(T.p6[:, 0:64], T.identf[:, :], T.t2s[:, :], True, False)])
-    m_b0 = wrap(T.p4[:, 0:64], T.zi, T.tag, W, [s_ta], start=False)
-    op("p", mm(T.p7[:, 0:64], T.identf[:, :], T.t3s[:, :], True, False), [s_t3s])
-    m_b3 = wrap(T.p7[:, 0:64], T.zo, T.ne3, W, [n3], start=False)
-    f2 = s_m0
-    for bank, m_b in ((T.p5, m_b1), (T.p6, m_b2), (T.p4, m_b0), (T.p7, m_b3)):
-        f2 = tt(T.mm[:, :], bank[:, 0:64], T.m0[:, :] if f2 == s_m0 else T.mm[:, :], A.min, [f2, m_b])
+    s_cf = act(T.cf[:, :], T.cc[:, 16 * ZV:W], [x_c, c_self], F.Copy, scale=64.0)
+    k_ids = act(T.idf[:, :], T.idlo[:, :], [k_idlo, k_pa], F.Identity, bias=T.pa[:, :])
+    m_v = wrap(T.p0[:, 0:24], T.za, T.fw, MISS, [w_hd, r1], a0=B)
+
+    def look(out, lst, a, b, deps):
+        return tt(out[:, 16 * a:16 * b], U.indirect(lst[:, a:b]), T.yw[:, S + 16 * a:S + 16 * b], A.subtract, deps)
+
+    def size(out, in_, a, b, deps):
+        return act(out[:, 16 * a:16 * b], in_[:, 16 * a:16 * b], deps, F.Abs)
+    ga0 = look(T.da, T.l0, 0, 32, [c_l0, c_pk0] + c_u)
+    m_l20 = wrap(T.p6[:, 0:32], T.zf, T.da, H, [ga0, k_zf])
+    ga1 = look(T.da, T.l0, 32, 64, [c_pk1])
+    m_l21 = wrap(T.p1[:, 0:32], T.zf, T.da, H, [ga1], a0=H)
+    aa0 = size(T.aa, T.da, 0, 32, [ga0])
+    c_l20 = cp(T.l2[:, 0:32], T.p6[:, 0:32], [m_l20])
+    c_lv = cp(T.lv[:, :], T.p0[:, 0:24], [m_v])
+    gb0 = look(T.db, T.l2, 0, 32, [c_l20])
+    aa1 = size(T.aa, T.da, 32, 64, [ga1])
+    s_l20 = act(T.l2f[:, 0:32], T.p6[:, 0:32], [c_l20], F.Copy, bias=-4096.0)
+    c_l21 = cp(T.l2[:, 32:64], T.p1[:, 0:32], [m_l21])
+    gb1 = look(T.db, T.l2, 32, 48, [c_l21])
+    gb2 = look(T.db, T.l2, 48, 64, [])
+    m_v0 = wrap(T.p4[:, 0:64], T.za, T.aa, W, [aa0, aa1, s_l0], start=False, before=[mm(T.p4[:, 0:64], T.identf[:, :], T.l0f[:, :], True, False)])
+    m_v1 = wrap(T.p5[:, 0:64], T.zb, T.aa, W, [k_zb])
+    ab0 = size(T.ab, T.db, 0, 32, [gb0])
+    s_l21 = act(T.l2f[:, 32:64], T.p1[:, 0:32], [c_l21], F.Copy, bias=-4096.0)
+    ab1 = size(T.ab, T.db, 32, 48, [gb1])
+    ab2 = size(T.ab, T.db, 48, 64, [gb2])
+    w_id = dma("y", T.yw[0:128:16, 0:S], T.idf[:, :], [gb0, gb1, gb2, k_ids])
+    op("p", mm(T.p2[:, 0:64], T.identf[:, :], T.l2f[:, :], True, False), [s_l20, s_l21])
+    m_v3 = wrap(T.p7[:, 0:64], T.zb, T.ab, W, [ab0, ab1, ab2])
+    m_v2 = wrap(T.p2[:, 0:64], T.za, T.ab, W, [], start=False)
+    f1 = s_m0
+    for bank, m_b in ((T.p4, m_v0), (T.p5, m_v1), (T.p7, m_v3)):
+        f1 = tt(T.mm[:, :], bank[:, 0:64], T.m0[:, :] if f1 == s_m0 else T.mm[:, :], A.min, [f1, m_b])
 
     off = float(8193 - VB - MISS * r)
-    f3 = ts(T.ms[:, :], T.mm[:, :], 4096.0, A.is_ge, [f2])
+    f2 = ts(T.uu[:, :], T.mm[:, :], 4096.0, A.is_lt, [f1], 1.0e29, A.mult)
+    fa = ts(T.mp[:, :], T.mm[:, :], 4096.0, A.min, [f1], off, A.add)
+    f3 = tt(T.ms[:, :], T.p2[:, 0:64], T.uu[:, :], A.is_ge, [f2, m_v2])
+    fb = ts(T.mq[:, :], T.p2[:, 0:64], 0.0, A.min, [m_v2], off + 4096.0, A.add)
     f4 = scan(T.s2[:, :], T.ones[:, 0:64], T.ms[:, :], 0.0, A.subtract, [f3])
-    f5 = ts(T.mo[:, :], T.mm[:, :], 4096.0, A.min, [f2], off, A.add)
+    f5 = tt(T.mo[:, :], T.mp[:, :], T.mq[:, :], A.min, [fa, fb])
     op("p", mm(T.p3[:, 0:64], T.nw[:, :], T.ms[:, :], True, False), [f3, k_nw, s_m0])
     m_n = op("p", mm(T.p3[:, 0:64], T.nb[:, :], T.s2[:, :], False, True), [f4])
     f6 = tt(T.uu[:, :], T.p3[:, 0:64], T.mo[:, :], A.max, [m_n, f5])
@@ -360,15 +413,16 @@ def rank_program(g, core, T, topo):
 
     wide = max(8 * (job[-1] - job[0] + 1) for job in me["jobs"][:2])
     assert all(8 * job[0] + wide <= 64 for job in me["jobs"][:2])
-    remote([xfer(topo, core, me["helpers"][k], me["e_on"][k], T.sem.qa, T.ix[:, 8 * me["jobs"][k][0]:8 * me["jobs"][k][0] + wide],
+    remote([xfer(topo, core, me["helpers"][k], me["e_feed"][k], T.sem.qa, T.ix[:, 8 * me["jobs"][k][0]:8 * me["jobs"][k][0] + wide],
                  T.h2[:, 0:wide]) for k in range(2)], [c_ix])
-    remote([xfer(topo, core, cores[q], me["e_near"][j], T.sem.rn, T.ix[:, 8 * q:8 * q + 8],
-                 T.an[:, 8 * lay[q]["order"].index(r):8 * lay[q]["order"].index(r) + 8]) for j, q in enumerate(near)], [c_ix])
+    remote([xfer(topo, core, cores[q], me["e_direct"][j], T.sem.rn, T.ix[:, 8 * q:8 * q + 8],
+                 T.an[:, 8 * lay[q]["order"].index(r):8 * lay[q]["order"].index(r) + 8]) for j, q in enumerate(direct)]
+           + [xfer(topo, core, me["helpers"][2], me["e_feed"][2], T.sem.qa, T.ix[:, 8 * third:8 * third + 8], T.h2[:, 0:8])], [c_ix])
 
-    m_v = wrap(T.p0[:, 0:24], T.z1f, T.yw, MISS, [w_va, k_z1f, r1], a0=VB + MISS * r)
-    h1 = cp(T.st[:, :].indirect(T.ix[:, :]), T.cc[:, :], [c_ix, k_mz, n2, n3, t_g0, t_g1a, t_g1b])
-    c_lv = cp(T.lv[:, :], T.p0[:, 0:24], [m_v])
-    h2 = cp(T.st[:, 0:S].indirect(T.lv[:, :]), mine, [h1, c_lv])
+    h1 = cp(T.st[:, :].indirect(T.ix[:, 0:ZV]), T.cc[:, 0:16 * ZV], [c_ix, k_mz])
+    h1s = act(T.sw[:, :].indirect(T.ix[:, ZV:64]), T.cf[:, :], [c_ix, s_cf, k_sz], F.Silu)
+    h1c = act(T.sb[:, :], mine_s, [h1s], F.Copy, scale=1.0 / 64)
+    h2 = tt(T.st[:, 0:S].indirect(T.lv[:, :]), mine, T.sb[:, :], A.add, [h1, h1c, c_lv])
     o_z = dma("y", T.z[:, :], T.st[:, 0:S], [h2])
 
     def block(b, lst):
@@ -376,12 +430,17 @@ def rank_program(g, core, T, topo):
 
     def vblock(b, lst):
         return lambda: V.tensor_scalar(T.ay[:, CAP * b:CAP * b + CAP], T.yw[:, :].indirect(lst), float(S * order[b]), None, A.add)
-    nf = len(far)
-    y0 = op("s", block(N - 1, T.ix[:, 8 * r:8 * r + 8]), [c_ix, w_va, k_yi])
-    y2 = op("s", [block(b, T.an[:, 8 * b:8 * b + 8]) for b in range(nf)], [x_f])
-    y3 = op("v", [vblock(b, T.an[:, 8 * b:8 * b + 8]) for b in range(nf, N - 1)], [x_n, w_va, k_yi])
-    y4 = act(T.yb[:, 0:384], T.ay[:, :].indirect(T.ld[:, 0:24]), [y0, y2, y3, b6])
-    y5 = cp(T.yb[:, 384:M], T.ay[:, :].indirect(T.ld[:, 24:48]), [y0, y2, y3, b6])
+
+    def got(b):
+        return T.an[:, 8 * b:8 * b + 8]
+    early = [order.index(q) for q in near if r in lay[q]["direct"]]
+    late = [b for b in range(N - 1) if b not in early]
+    y0 = op("s", block(N - 1, T.ix[:, 8 * r:8 * r + 8]), [c_ix, w_va, w_id])
+    y1 = op("s", [block(b, got(b)) for b in early], [x_n])
+    y2 = op("s", [block(b, got(b)) for b in late[:3]], [x_f])
+    y3 = op("v", [vblock(b, got(b)) for b in late[3:]], [x_f, w_va, w_id])
+    y4 = act(T.yb[:, 0:384], T.ay[:, :].indirect(T.ld[:, 0:24]), [y0, y1, y2, y3, b6])
+    y5 = cp(T.yb[:, 384:M], T.ay[:, :].indirect(T.ld[:, 24:48]), [y0, y1, y2, y3, b6])
     o_y = dma("s", T.y[:, :], T.yb[0:128:16, :], [y4, y5])
     op("s", [], [o_y])
     op("y", [], [o_z])

from concourse.bass import DstId, RemoteDMATransfer
from concourse.mybir import AluOpType as A, ActivationFunctionType as F

N, M, S, B, CAP, MISS = 8, 768, 3072, 2048, 128, 384
W = N * CAP
VB = S + W
R = S // 16
BANK = 512
FA, JV, HV, ZV = 2048, 104, 32, 38
NCS, NDS = 70, 24

SCRATCH = {
    "ch": ("sbuf", [128, M], "bfloat16"), "wc": ("sbuf", [128, 1], "float32"),
    "st": ("sbuf", [128, VB + N * MISS], "bfloat16"),
    "hd": ("sbuf", [128, 152], "int32"), "fo": ("sbuf", [128, R], "int32"), "va": ("sbuf", [128, 24], "int32"),
    "ones": ("sbuf", [128, 256], "bfloat16"), "mones": ("sbuf", [128, 128], "bfloat16"),
    "xs": ("sbuf", [128, W], "bfloat16"), "fw": ("sbuf", [128, S], "bfloat16"), "rm": ("sbuf", [128, 384], "bfloat16"),
    "dd": ("sbuf", [128, 144], "bfloat16"), "zw": ("sbuf", [128, 144], "bfloat16"),
    "zf": ("sbuf", [128, 144], "bfloat16"), "za": ("sbuf", [128, 144], "bfloat16"), "zb": ("sbuf", [128, 144], "bfloat16"),
    "pk": ("sbuf", [128, 144], "bfloat16"), "pj": ("sbuf", [128, 128], "bfloat16"),
    "nb": ("sbuf", [128, 128], "bfloat16"), "nt": ("sbuf", [128, 128], "bfloat16"),
    "nw": ("sbuf", [128, 128], "bfloat16"),
    "ident": ("sbuf", [128, 128], "bfloat16"), "identf": ("sbuf", [128, 128], "float32"),
    "kq": ("sbuf", [128, 384], "bfloat16"),
    "pi": ("sbuf", [128, 1], "int32"), "pr": ("sbuf", [128, 1], "float32"),
    "pf": ("sbuf", [128, 1], "float32"), "pl": ("sbuf", [128, 1], "float32"),
    "pa": ("sbuf", [128, 1], "float32"), "pb": ("sbuf", [128, 1], "float32"),
    "idhi": ("sbuf", [128, R], "bfloat16"), "idlo": ("sbuf", [128, R], "bfloat16"), "idf": ("sbuf", [128, R], "float32"),
    "fhb": ("sbuf", [128, R], "bfloat16"), "flb": ("sbuf", [128, R], "bfloat16"),
    "hhb": ("sbuf", [128, 152], "bfloat16"), "hlb": ("sbuf", [128, 152], "bfloat16"),
    "lf": ("sbuf", [128, R], "uint16"),
    "vf": ("sbuf", [128, 24 * N], "float32"), "vl": ("sbuf", [128, 24 * N], "int32"),
    "x1": ("sbuf", [128, 48], "int32"), "own": ("sbuf", [128, 48], "int32"),
    "mk": ("sbuf", [128, 384], "bfloat16"), "sm": ("sbuf", [128, 384], "bfloat16"), "dm": ("sbuf", [128, 384], "float16"),
    "ld": ("sbuf", [128, 48], "uint16"),
    "cc": ("sbuf", [128, W], "bfloat16"),
    "gs": ("sbuf", [128, S], "bfloat16"), "gj": ("sbuf", [128, S], "bfloat16"),
    "ji": ("sbuf", [128, 64], "float32"),
    "x2": ("sbuf", [128, 64], "int32"), "ba": ("sbuf", [128, 64], "int32"), "lb": ("sbuf", [128, 64], "uint16"),
    "l0": ("sbuf", [128, 64], "uint16"), "l2": ("sbuf", [128, 64], "uint16"),
    "l0f": ("sbuf", [128, 64], "float32"), "l2f": ("sbuf", [128, 64], "float32"),
    "hg": ("sbuf", [128, W], "bfloat16"),
    "da": ("sbuf", [128, W], "bfloat16"), "db": ("sbuf", [128, W], "bfloat16"),
    "aa": ("sbuf", [128, W], "bfloat16"), "ab": ("sbuf", [128, W], "bfloat16"),
    "mm": ("sbuf", [128, 64], "float32"), "rr": ("sbuf", [128, 64], "float32"), "m0": ("sbuf", [128, 64], "float32"),
    "mo": ("sbuf", [128, 64], "float32"), "uu": ("sbuf", [128, 64], "float32"),
    "ms": ("sbuf", [128, 64], "bfloat16"), "s2": ("sbuf", [128, 64], "bfloat16"),
    "ix": ("sbuf", [128, 64], "uint16"), "lv": ("sbuf", [128, 24], "uint16"), "an": ("sbuf", [128, 64], "uint16"),
    "yw": ("sbuf", [128, VB + N * MISS], "float32"),
    "sw": ("sbuf", [128, VB + N * MISS], "float32"), "cf": ("sbuf", [128, W - 16 * ZV], "float32"), "sb": ("sbuf", [128, MISS], "bfloat16"),
    "mp": ("sbuf", [128, 64], "float32"), "mq": ("sbuf", [128, 64], "float32"),
    "ay": ("sbuf", [128, W], "float32"), "yb": ("sbuf", [128, M], "float32"),
    "h1": ("sbuf", [128, 2 * CAP], "bfloat16"), "h2": ("sbuf", [128, 64], "uint16"),
    "p0": ("psum", [128, 512], "float32"), "p1": ("psum", [128, 512], "float32"),
    "p2": ("psum", [128, 512], "float32"), "p3": ("psum", [128, 512], "float32"),
    "p4": ("psum", [128, 512], "float32"), "p5": ("psum", [128, 512], "float32"),
    "p6": ("psum", [128, 512], "float32"), "p7": ("psum", [128, 512], "float32"),
}
SEMAPHORES = (["ls", "rv", "rc", "rn", "rf", "qv", "qc", "qa"]
              + ["c%d" % i for i in range(NCS)] + ["d%d" % i for i in range(NDS)])


def bits(engines):
    m = 0
    for e in engines:
        m |= 1 << e
    return m


def share(engines, n):
    k = 1
    while 2 * k * n <= len(engines):
        k *= 2
    out = [engines[i * k:(i + 1) * k] for i in range(n)]
    if len(engines) - n * k >= k:
        out[-1] = out[-1] + engines[n * k:(n + 1) * k]
    return out


def layout(cores, r, topo):
    c = cores[r]
    near = [q for q in range(N) if q != r and topo.may_write(c, cores[q])]
    far = [q for q in range(N) if q != r and q not in near]
    cand = sorted([h for h in topo.cores_of(c) if h not in cores], key=lambda h: (topo.die(h) != topo.die(c), h))
    helpers = [h for h in cand if all(topo.may_write(h, cores[q]) for q in far)][:2]
    helpers.append([h for h in cand if h not in helpers and all(topo.may_write(h, cores[q]) for q in near)][0])
    on, off = topo.engines(c, helpers[0]), topo.engines(c, cores[near[0]])
    half = len(far) // 2
    third = min(near, key=lambda q: (q - r) % N)
    direct = [q for q in near if q != third]
    jobs = [far[:half], far[half:], [third]]
    vjobs = [far[:half], far[half:], near]
    return {"near": near, "far": far, "direct": direct, "helpers": helpers, "jobs": jobs, "vjobs": vjobs, "order": far + near + [r],
            "e_direct": share(off, len(direct)), "e_feed": share(on, 2) + [[e for e in on if e not in off]], "e_vac": share(on, 3),
            "e_help": [share(topo.engines(helpers[k], cores[jobs[k][0]]), len(jobs[k])) for k in range(3)],
            "e_vhelp": [share(topo.engines(helpers[k], cores[vjobs[k][0]]), len(vjobs[k])) for k in range(3)]}


def xfer(topo, src_core, dst_core, engines, sem, src, dst):
    rid, pid = topo.addr(dst_core, src_core)
    return RemoteDMATransfer(dst_ids=[DstId(rid=rid, pnc=pid)], dma_engine_mask=bits(engines), remote_sem=sem, src=src, dst=dst)


def helper_program(g, core, T, topo, lay, r, k):
    cores, me = T.cores, lay[r]
    job, eng = me["jobs"][k], me["e_help"][k]
    g.wait_ge(T.sem.qv, len(me["e_vac"][k]))
    g.remote_dma_fused([xfer(topo, core, cores[q], me["e_vhelp"][k][j], T.sem.rv, T.va[:, :], T.vl[:, 24 * r:24 * r + 24])
                        for j, q in enumerate(me["vjobs"][k])], local_sem=T.sem.ls)
    got = len(me["e_feed"][k])
    g.wait_ge(T.sem.qc, got)
    g.remote_dma_fused([xfer(topo, core, cores[q], eng[j], T.sem.rc, T.h1[:, CAP * j:CAP * j + CAP], T.cc[:, CAP * r:CAP * r + CAP])
                        for j, q in enumerate(job)], local_sem=T.sem.ls)
    g.wait_ge(T.sem.qa, got)
    tr = []
    for j, q in enumerate(job):
        a, b = 8 * (q - job[0]), 8 * lay[q]["order"].index(r)
        tr.append(xfer(topo, core, cores[q], eng[j], T.sem.rf, T.h2[:, a:a + 8], T.an[:, b:b + 8]))
    g.remote_dma_fused(tr, local_sem=T.sem.ls)
    g.wait_ge(T.sem.ls, 2 * sum(len(e) for e in eng) + sum(len(e) for e in me["e_vhelp"][k]))


def emit(ops, queues, T):
    known = {q: set() for q in queues}
    snap, waits, needed = [], [], set()
    for i, o in enumerate(ops):
        kn, w = known[o["q"]], []
        for d in sorted(set(o["deps"]), reverse=True):
            if d not in kn:
                w.append(d)
                kn.add(d)
                kn |= snap[d]
        needed.update(w)
        waits.append(w)
        snap.append(set(kn) if o["q"] else set())
    pools = {True: [], False: []}
    sig = {}
    for i, o in enumerate(ops):
        if o["q"] is None:
            sig[i] = o["ext"]
            continue
        q = queues[o["q"]]
        for d in waits[i]:
            q.wait_ge(T.sem[sig[d][0]], sig[d][1])
        slot = None
        if i in needed:
            pool = pools[o["dma"]]
            for s in pool:
                if s[1] in snap[i]:
                    slot = s
                    break
            if slot is None:
                slot = [("d%d" if o["dma"] else "c%d") % len(pool), i, 0]
                pool.append(slot)
            slot[1] = i
        for n, fn in enumerate(o["fns"]):
            ins = fn()
            if slot is not None and (not o["acc"] or n == len(o["fns"]) - 1):
                inc = 16 if o["dma"] else 1
                ins.then_inc(T.sem[slot[0]], inc)
                slot[2] += inc
        if slot is not None:
            sig[i] = (slot[0], slot[2])


def rank_program(g, core, T, topo):
    cores = T.cores
    lay = [layout(cores, r, topo) for r in range(N)]
    r = T.rank_of(core)
    if r is None:
        for q in range(N):
            if core in lay[q]["helpers"]:
                helper_program(g, core, T, topo, lay, q, lay[q]["helpers"].index(core))
        return
    me = lay[r]
    order, near, far, direct = me["order"], me["near"], me["far"], me["direct"]
    V, Sc, PE, Sy = g.vector, g.scalar, g.tensor, g.sync
    queues = {"g": g, "v": V, "s": Sc, "p": PE, "y": Sy, None: None}
    ops = []

    def op(q, fns, deps=(), dma=False, acc=False):
        ops.append({"q": q, "fns": fns if isinstance(fns, list) else [fns], "deps": list(deps), "dma": dma, "acc": acc})
        return len(ops) - 1

    def ext(name, val):
        ops.append({"q": None, "fns": [], "deps": [], "ext": (name, val)})
        return len(ops) - 1

    def dma(q, out, in_, deps=()):
        return op(q, lambda: queues[q].dma_start(out, in_), deps, dma=True)

    def dmas(q, pairs, deps=()):
        return op(q, [(lambda o=o, i=i: queues[q].dma_start(o, i)) for o, i in pairs], deps, dma=True)

    def ts(out, in0, s1, op0, deps, s2=None, op1=None):
        if op1 is None:
            return op("v", lambda: V.tensor_scalar(out, in0, s1, None, op0), deps)
        return op("v", lambda: V.tensor_scalar(out, in0, s1, s2, op0, op1), deps)

    def tt(out, in0, in1, o, deps):
        return op("v", lambda: V.tensor_tensor(out, in0, in1, o), deps)

    def cp(out, in_, deps):
        return op("v", lambda: V.tensor_copy(out, in_), deps)

    def scan(out, d0, d1, init, o1, deps):
        return op("v", lambda: V.tensor_tensor_scan(out, d0, d1, init, A.mult, o1), deps)

    def fill(ap, val, deps=()):
        return op("v", lambda: V.memset(ap, val), deps)

    def act(out, in_, deps, func=F.Copy, **kw):
        return op("s", lambda: Sc.activation(out, in_, func, **kw), deps)

    def move(q, out, in_, deps):
        return cp(out, in_, deps) if q == "v" else act(out, in_, deps)

    def sel(out, in_, pattern, cmp, fillv, base, cm, deps):
        return op("g", lambda: g.affine_select(out, in_, pattern, cmp, fillv, base, cm), deps)

    def iota(out, pattern, base, cm):
        return op("g", lambda: g.iota(out, pattern, base, cm, allow_small_or_imprecise_dtypes=True))

    def mm(out, lhsT, rhs, start, stop):
        return lambda: PE.matmul(out, lhsT, rhs, start, stop)

    def wrap(out, z, src, n, deps, start=True, stop=True, before=(), a0=0):
        fns = list(before) + [mm(out, z[:, 15 - i:143 - i], src[:, a0 + i:a0 + n:16], start and i == 0, stop and i == 15) for i in range(16)]
        return op("p", fns, deps, acc=True)

    def remote(transfers, deps):
        return op("g", lambda: g.remote_dma_fused(transfers, local_sem=T.sem.ls), deps)

    def landing(key, jobs):
        return sum(len(lay[q][key][k][lay[q][jobs][k].index(r)]) for q in range(N) for k in range(3) if r in lay[q][jobs][k])

    n_near = sum(len(lay[q]["e_direct"][lay[q]["direct"].index(r)]) for q in near if r in lay[q]["direct"])
    n_far = landing("e_help", "jobs")
    x_v = ext("rv", landing("e_vhelp", "vjobs"))
    x_c, x_n, x_f = ext("rc", n_near + n_far), ext("rn", n_near), ext("rf", n_far)
    x_l = ext("ls", sum(len(e) for e in me["e_vac"]) + 2 * (sum(len(e) for e in me["e_direct"]) + sum(len(e) for e in me["e_feed"])))

    l_wt = dma("y", T.wc[:, :], T.wt[:, :])
    l_va = dma("s", T.vl[:, 24 * r:24 * r + 24], T.vac[:, :])
    l_ch = dma("y", T.ch[:, :], T.chunks[:, :])
    l_fo = dma("y", T.fo[:, :], T.follow[:, :])
    l_st = dma("y", T.st[:, 0:S], T.store[:, :])
    l_hd = dmas("y", [(T.hd[:, 0:128], T.head[:, :]), (T.hd[:, 128:152], T.vac[:, :])])

    upto, from_ = [[16, 9], [0, 16]], [[-16, 9], [0, 16]]
    k_p = iota(T.pf[:, :], [[0, 1]], 0, 1)
    k_mon = fill(T.mones[:, :], -1.0)
    k_one = fill(T.ones[:, :], 1.0)
    k_gi = ts(T.pi[:, :], T.pf[:, :], 0.0625, A.mult, [k_p], -0.46875, A.add)
    k_idlo = scan(T.idlo[:, :], T.ones[:, 0:R], T.ones[:, 0:R], -1.0, A.add, [k_one])
    k_pl = ts(T.pl[:, :], T.pi[:, :], 16.0, A.mult, [k_gi], 15.0, A.add)
    k_pk0 = fill(T.pk[:, :], 0.0)
    k_fwa = fill(T.fw[:, 0:FA], 0.0)
    k_nt0 = sel(T.nt[:, :], T.mones[:, :], [[-1, 128]], A.is_ge, 0.0, 0, 1, [k_mon])
    k_nb0 = sel(T.nb[:, :], T.mones[:, :], [[-16, 8], [0, 16]], A.is_ge, 0.0, 0, 1, [k_mon])
    k_nt = sel(T.nt[:, :], T.nt[:, :], [[16, 8], [0, 16]], A.is_ge, 0.0, 15, -1, [k_nt0])
    k_nb = sel(T.nb[:, :], T.nb[:, :], [[16, 8], [0, 16]], A.is_ge, 0.0, 15, -1, [k_nb0])
    k_xs = op("s", [(lambda a=a: Sc.activation(T.xs[:, a:a + 256], T.ones[:, :], F.Copy, scale=-1.0)) for a in range(0, W, 256)], [k_one])
    k_pr = act(T.pr[:, :], T.pl[:, :], [k_pl], F.Identity, bias=T.pf[:, :], scale=-1.0)
    k_kq = op("s", [(lambda b=b: Sc.activation(T.kq[:, 48 * b:48 * b + 48], T.ones[:, 0:48], F.Copy, scale=-8.0 * b)) for b in range(N)], [k_one])
    k_pa = act(T.pa[:, :], T.pr[:, :], [k_pr], F.Identity, bias=15.0 * R, scale=float(R))
    k_pb = act(T.pb[:, :], T.pr[:, :], [k_pr], F.Identity, bias=15.0 * 64 + S, scale=64.0)
    k_idhi = act(T.idhi[:, :], T.ones[:, 0:R], [k_pa], F.Identity, bias=T.pa[:, :], scale=0.0)
    mine, mine_s = T.st[:, VB + MISS * r:VB + MISS * (r + 1)], T.sw[:, VB + MISS * r:VB + MISS * (r + 1)]
    k_sz = act(mine_s, T.xs[:, 0:MISS], [k_xs], F.Silu, scale=0.0)
    k_zw = ts(T.zw[:, :], T.idlo[:, 0:144], T.pl[:, :], A.is_equal, [k_idlo, k_pl, l_wt], T.wc[:, :], A.mult)
    k_rm0 = fill(T.rm[:, :], 1.0)
    k_fw = fill(T.fw[:, FA:S], 0.0)

    remote([xfer(topo, core, me["helpers"][k], me["e_vac"][k], T.sem.qv, T.vl[:, 24 * r:24 * r + 24], T.va[:, :]) for k in range(3)], [l_va])
    k_pk = k_pk0
    for k in range(3):
        k_pk = sel(T.pk[:, :], T.pk[:, :], [[-16, 9], [-3, 16]], A.not_equal, 4096.0 * 256 ** k, 30 - k, 1, [k_pk])
    k_pk = sel(T.pk[:, :], T.pk[:, :], upto, A.is_ge, 0.0, 15, -1, [k_pk])
    k_pk = sel(T.pk[:, :], T.pk[:, :], from_, A.is_ge, 0.0, 0, 1, [k_pk])
    pk_a, pk_b = T.pk[:, 0:128], T.pk[:, 6:134]

    m_s1 = wrap(T.p0[:, 0:48], T.zw, T.ch, M, [k_zw, l_ch])
    b1 = ts(T.x1[:, :], T.p0[:, 0:48], 13.0, A.mult, [m_s1])
    k_rm = fill(T.rm[:, 0:384:48], 0.0, [k_rm0])
    b2 = ts(T.own[:, :], T.x1[:, :], 2, A.arith_shift_right, [b1], 7, A.bitwise_and)
    k_id = ts(T.ident[:, :], T.idlo[:, 0:128], T.pf[:, :], A.is_equal, [k_idlo])
    b3 = op("v", [(lambda b=b: V.tensor_scalar(T.mk[:, 48 * b:48 * b + 48], T.own[:, :], float(order[b]), None, A.is_equal)) for b in range(N)], [b2])
    b4 = scan(T.sm[:, :], T.rm[:, :], T.mk[:, :], 0.0, A.subtract, [b3, k_rm])
    c_lf = cp(T.lf[:, :], T.fo[:, :], [l_fo])
    op("p", mm(T.p1[:, 0:384], T.nt[:, :], T.mk[:, :], True, False), [k_nt, b3])
    op("p", mm(T.p1[:, 0:384], T.nb[:, :], T.kq[:, :], False, False), [k_nb, k_kq])
    m_pos = op("p", mm(T.p1[:, 0:384], T.nb[:, :], T.sm[:, :], False, True), [b4])
    a1 = cp(T.fhb[:, :], T.fo[:, :], [l_fo])
    b5 = tt(T.dm[:, :], T.p1[:, 0:384], T.mk[:, :], A.mult, [m_pos])
    m_de = op("p", [mm(T.p0[:, 0:48], T.ident[:, :], T.dm[:, 48 * b:48 * b + 48], b == 0, b == N - 1) for b in range(N)], [b5, k_id, b1], acc=True)
    a2 = tt(T.flb[:, :], T.fo[:, :], T.fhb[:, :], A.subtract, [a1])
    w_fo = dmas("y", [(T.fw[3:128:16, :], T.idlo[:, :]), (T.fw[2:128:16, :], T.idhi[:, :]),
                      (T.fw[0:128:16, :], T.fhb[:, :]), (T.fw[1:128:16, :], T.flb[:, :])], [k_fwa, k_fw, k_idlo, k_idhi, a1, a2])
    b6 = cp(T.ld[:, :], T.p0[:, 0:48], [m_de])
    b7 = cp(T.xs[:, :].indirect(T.ld[:, :]), T.ch[:, :], [b6, k_xs, k_sz])

    def blk(q):
        return T.xs[:, CAP * order.index(q):CAP * order.index(q) + CAP]
    third = me["jobs"][2][0]
    remote([xfer(topo, core, me["helpers"][k], me["e_feed"][k], T.sem.qc, T.xs[:, 2 * CAP * k:2 * CAP * (k + 1)], T.h1[:, :]) for k in range(2)], [b7])
    remote([xfer(topo, core, cores[q], me["e_direct"][j], T.sem.rc, blk(q), T.cc[:, CAP * r:CAP * r + CAP]) for j, q in enumerate(direct)]
           + [xfer(topo, core, me["helpers"][2], me["e_feed"][2], T.sem.qc, blk(third), T.h1[:, 0:CAP])], [b7])

    banks = [T.p2, T.p3, T.p4, T.p5, T.p6, T.p7]
    t_g = act(T.gs[:, :], T.st[:, 0:S].indirect(T.lf[:, :]), [l_st, c_lf])
    c_self = cp(T.cc[:, CAP * r:CAP * r + CAP], T.xs[:, W - CAP:W], [b7])
    k_dd = ts(T.dd[:, :], T.idlo[:, 0:144], T.pl[:, :], A.is_equal, [])
    a3 = cp(T.hhb[:, :], T.hd[:, :], [l_hd])
    t_jv = cp(T.gj[:, 0:16 * JV], T.fw[:, :].indirect(T.lf[:, 0:JV]), [w_fo, c_lf])
    t_js = act(T.gj[:, 16 * JV:S], T.fw[:, :].indirect(T.lf[:, JV:R]), [w_fo, c_lf])
    a4 = tt(T.hlb[:, :], T.hd[:, :], T.hhb[:, :], A.subtract, [a3])
    w_hd = dmas("y", [(T.fw[10:128:16, 0:B], T.hhb[:, 0:128]), (T.fw[11:128:16, 0:B], T.hlb[:, 0:128]),
                      (T.fw[10:128:16, B:B + MISS], T.hhb[:, 128:152]), (T.fw[11:128:16, B:B + MISS], T.hlb[:, 128:152])], [a3, a4, t_jv, t_js])
    k_pj = sel(T.pj[:, :], T.ident[:, :], [[16, 8], [0, 16]], A.is_ge, 0.0, 3, -1, [k_id])

    def unperm(k, lhsT, src, stop):
        fns, a = [], BANK * k
        while a < BANK * (k + 1):
            i, c0 = divmod(a, R)
            n = min(R - c0, BANK * (k + 1) - a)
            fns.append((banks[k][:, a - BANK * k:a - BANK * k + n], src[:, 16 * c0 + i:16 * (c0 + n - 1) + i + 1:16]))
            a += n
        return [mm(o, lhsT, s, False, stop and j == len(fns) - 1) for j, (o, s) in enumerate(fns)]
    op("p", [mm(banks[k][:, :], pk_a, T.st[:, BANK * k:BANK * (k + 1)], True, False) for k in range(6)], [k_pk, l_st], acc=True)
    op("p", [f for k in range(6) for f in unperm(k, pk_b, T.gs, False)], [t_g], acc=True)
    m_u = [op("p", unperm(k, T.pj[:, :], T.gj, True), [t_jv, t_js, k_pj], acc=True) for k in range(6)]
    c_u = [move("vs"[k % 2], T.yw[:, BANK * k:BANK * (k + 1)], banks[k][:, :], [m_u[k]]) for k in range(6)]

    k_za = sel(T.za[:, :], T.dd[:, :], from_, A.is_ge, 0.0, -10, 1, [k_dd])
    k_zf = sel(T.zf[:, :], T.dd[:, :], upto, A.is_ge, 0.0, 1, -1, [k_dd])
    k_zb0 = sel(T.zb[:, :], T.dd[:, :], upto, A.is_ge, 0.0, 9, -1, [k_dd])
    k_nw = sel(T.nw[:, :], T.nt[:, :], [[-1, 128]], A.not_equal, 8192.0, 0, 1, [k_nt])
    k_zb = sel(T.zb[:, :], T.zb[:, :], from_, A.is_ge, 0.0, -2, 1, [k_zb0])
    k_yv = op("g", [(lambda a=a: g.iota(T.yw[:, VB + a:VB + a + W], [[0, W]], 0, 0, allow_small_or_imprecise_dtypes=True)) for a in range(0, N * MISS, W)])
    k_idf = act(T.identf[:, :], T.ident[:, :], [k_id])
    k_ji = act(T.ji[:, :], T.idlo[:, 0:64], [k_idlo, k_pb], F.Identity, bias=T.pb[:, :])

    H = W // 2
    U = T.yw[:, 0:S]
    m_s2 = wrap(T.p0[:, 0:64], T.zw, T.cc, W, [x_c, c_self, b6])
    m_pk = [op("p", [mm(bank[:, :], pk_a, T.cc[:, H * h:H * (h + 1)], True, False), mm(bank[:, :], pk_b, T.cc[:, H * h:H * (h + 1)], False, True)],
               [b5, c_u[0]], acc=True) for h, bank in enumerate((T.p1, T.p2))]
    e1 = ts(T.x2[:, :], T.p0[:, 0:64], 13.0, A.mult, [m_s2])
    r1 = act(T.rr[:, :], T.p0[:, 0:64], [e1], F.Relu, scale=4096.0)
    e2 = ts(T.ba[:, :], T.x2[:, :], 5, A.arith_shift_right, [e1], B - 1, A.bitwise_and)
    c_lb = cp(T.lb[:, :], T.ba[:, :], [e2])
    s_hv = cp(T.hg[:, 0:16 * HV], T.fw[:, 0:B].indirect(T.lb[:, 0:HV]), [c_lb, w_hd])
    s_hs = act(T.hg[:, 16 * HV:W], T.fw[:, 0:B].indirect(T.lb[:, HV:64]), [c_lb, w_hd])
    m_m0 = op("p", [mm(T.p3[:, 0:64], T.identf[:, :], T.ji[:, :], True, False), mm(T.p3[:, 0:64], T.identf[:, :], T.rr[:, :], False, True)],
              [r1, k_ji, k_idf, c_u[1]], acc=True)
    m_l0 = wrap(T.p4[:, 0:64], T.za, T.hg, W, [s_hv, s_hs, k_za, c_u[2]])
    c_pk0 = act(T.yw[:, S:S + H], T.p1[:, :], [m_pk[0]])
    c_pk1 = act(T.yw[:, S + H:S + W], T.p2[:, :], [m_pk[1]])
    k_mz = fill(mine, 0.0)
    c_vf = cp(T.vf[:, :], T.vl[:, :], [l_va, x_v])
    w_va = dmas("y", [(T.yw[0:128:16, VB + MISS * q:VB + MISS * (q + 1)], T.vf[:, 24 * q:24 * q + 24]) for q in range(N)], [k_yv, c_vf])
    c_l0 = cp(T.l0[:, :], T.p4[:, 0:64], [m_l0])
    s_l0 = act(T.l0f[:, :], T.p4[:, 0:64], [c_l0])
    s_m0 = act(T.m0[:, :], T.p3[:, 0:64], [m_m0])
    s_cf = act(T.cf[:, :], T.cc[:, 16 * ZV:W], [x_c, c_self], F.Copy, scale=64.0)
    k_ids = act(T.idf[:, :], T.idlo[:, :], [k_idlo, k_pa], F.Identity, bias=T.pa[:, :])
    m_v = wrap(T.p0[:, 0:24], T.za, T.fw, MISS, [w_hd, r1], a0=B)

    def look(out, lst, a, b, deps):
        return tt(out[:, 16 * a:16 * b], U.indirect(lst[:, a:b]), T.yw[:, S + 16 * a:S + 16 * b], A.subtract, deps)

    def size(out, in_, a, b, deps):
        return act(out[:, 16 * a:16 * b], in_[:, 16 * a:16 * b], deps, F.Abs)
    ga0 = look(T.da, T.l0, 0, 32, [c_l0, c_pk0] + c_u)
    m_l20 = wrap(T.p6[:, 0:32], T.zf, T.da, H, [ga0, k_zf])
    ga1 = look(T.da, T.l0, 32, 64, [c_pk1])
    m_l21 = wrap(T.p1[:, 0:32], T.zf, T.da, H, [ga1], a0=H)
    aa0 = size(T.aa, T.da, 0, 32, [ga0])
    c_l20 = cp(T.l2[:, 0:32], T.p6[:, 0:32], [m_l20])
    c_lv = cp(T.lv[:, :], T.p0[:, 0:24], [m_v])
    gb0 = look(T.db, T.l2, 0, 32, [c_l20])
    aa1 = size(T.aa, T.da, 32, 64, [ga1])
    s_l20 = act(T.l2f[:, 0:32], T.p6[:, 0:32], [c_l20], F.Copy, bias=-4096.0)
    c_l21 = cp(T.l2[:, 32:64], T.p1[:, 0:32], [m_l21])
    gb1 = look(T.db, T.l2, 32, 48, [c_l21])
    gb2 = look(T.db, T.l2, 48, 64, [])
    m_v0 = wrap(T.p4[:, 0:64], T.za, T.aa, W, [aa0, aa1, s_l0], start=False, before=[mm(T.p4[:, 0:64], T.identf[:, :], T.l0f[:, :], True, False)])
    m_v1 = wrap(T.p5[:, 0:64], T.zb, T.aa, W, [k_zb])
    ab0 = size(T.ab, T.db, 0, 32, [gb0])
    s_l21 = act(T.l2f[:, 32:64], T.p1[:, 0:32], [c_l21], F.Copy, bias=-4096.0)
    ab1 = size(T.ab, T.db, 32, 48, [gb1])
    ab2 = size(T.ab, T.db, 48, 64, [gb2])
    w_id = dma("y", T.yw[0:128:16, 0:S], T.idf[:, :], [gb0, gb1, gb2, k_ids])
    op("p", mm(T.p2[:, 0:64], T.identf[:, :], T.l2f[:, :], True, False), [s_l20, s_l21])
    m_v3 = wrap(T.p7[:, 0:64], T.zb, T.ab, W, [ab0, ab1, ab2])
    m_v2 = wrap(T.p2[:, 0:64], T.za, T.ab, W, [], start=False)
    f1 = s_m0
    for bank, m_b in ((T.p4, m_v0), (T.p5, m_v1), (T.p7, m_v3)):
        f1 = tt(T.mm[:, :], bank[:, 0:64], T.m0[:, :] if f1 == s_m0 else T.mm[:, :], A.min, [f1, m_b])

    off = float(8193 - VB - MISS * r)
    f2 = ts(T.uu[:, :], T.mm[:, :], 4096.0, A.is_lt, [f1], 1.0e29, A.mult)
    fa = ts(T.mp[:, :], T.mm[:, :], 4096.0, A.min, [f1], off, A.add)
    f3 = tt(T.ms[:, :], T.p2[:, 0:64], T.uu[:, :], A.is_ge, [f2, m_v2])
    fb = ts(T.mq[:, :], T.p2[:, 0:64], 0.0, A.min, [m_v2], off + 4096.0, A.add)
    f4 = scan(T.s2[:, :], T.ones[:, 0:64], T.ms[:, :], 0.0, A.subtract, [f3])
    f5 = tt(T.mo[:, :], T.mp[:, :], T.mq[:, :], A.min, [fa, fb])
    op("p", mm(T.p3[:, 0:64], T.nw[:, :], T.ms[:, :], True, False), [f3, k_nw, s_m0])
    m_n = op("p", mm(T.p3[:, 0:64], T.nb[:, :], T.s2[:, :], False, True), [f4])
    f6 = tt(T.uu[:, :], T.p3[:, 0:64], T.mo[:, :], A.max, [m_n, f5])
    c_ix = ts(T.ix[:, :], T.uu[:, :], off, A.subtract, [f6])

    wide = max(8 * (job[-1] - job[0] + 1) for job in me["jobs"][:2])
    assert all(8 * job[0] + wide <= 64 for job in me["jobs"][:2])
    remote([xfer(topo, core, me["helpers"][k], me["e_feed"][k], T.sem.qa, T.ix[:, 8 * me["jobs"][k][0]:8 * me["jobs"][k][0] + wide],
                 T.h2[:, 0:wide]) for k in range(2)], [c_ix])
    remote([xfer(topo, core, cores[q], me["e_direct"][j], T.sem.rn, T.ix[:, 8 * q:8 * q + 8],
                 T.an[:, 8 * lay[q]["order"].index(r):8 * lay[q]["order"].index(r) + 8]) for j, q in enumerate(direct)]
           + [xfer(topo, core, me["helpers"][2], me["e_feed"][2], T.sem.qa, T.ix[:, 8 * third:8 * third + 8], T.h2[:, 0:8])], [c_ix])

    h1 = cp(T.st[:, :].indirect(T.ix[:, 0:ZV]), T.cc[:, 0:16 * ZV], [c_ix, k_mz])
    h1s = act(T.sw[:, :].indirect(T.ix[:, ZV:64]), T.cf[:, :], [c_ix, s_cf, k_sz], F.Silu)
    h1c = act(T.sb[:, :], mine_s, [h1s], F.Copy, scale=1.0 / 64)
    h2 = tt(T.st[:, 0:S].indirect(T.lv[:, :]), mine, T.sb[:, :], A.add, [h1, h1c, c_lv])
    o_z = dma("y", T.z[:, :], T.st[:, 0:S], [h2])

    def block(b, lst):
        return lambda: Sc.activation(T.ay[:, CAP * b:CAP * b + CAP], T.yw[:, :].indirect(lst), F.Identity, bias=float(S * order[b]))

    def vblock(b, lst):
        return lambda: V.tensor_scalar(T.ay[:, CAP * b:CAP * b + CAP], T.yw[:, :].indirect(lst), float(S * order[b]), None, A.add)

    def got(b):
        return T.an[:, 8 * b:8 * b + 8]
    early = [order.index(q) for q in near if r in lay[q]["direct"]]
    late = [b for b in range(N - 1) if b not in early]
    y0 = op("s", block(N - 1, T.ix[:, 8 * r:8 * r + 8]), [c_ix, w_va, w_id])
    y1 = op("s", [block(b, got(b)) for b in early], [x_n])
    y2 = op("s", [block(b, got(b)) for b in late[:3]], [x_f])
    y3 = op("v", [vblock(b, got(b)) for b in late[3:]], [x_f, w_va, w_id])
    y4 = act(T.yb[:, 0:384], T.ay[:, :].indirect(T.ld[:, 0:24]), [y0, y1, y2, y3, b6])
    y5 = cp(T.yb[:, 384:M], T.ay[:, :].indirect(T.ld[:, 24:48]), [y0, y1, y2, y3, b6])
    o_y = dma("s", T.y[:, :], T.yb[0:128:16, :], [y4, y5])
    op("s", [], [o_y])
    op("y", [], [o_z])
    op("g", [], [x_l])
    emit(ops, queues, T)
